import numpy as np
import ml_dtypes


def mxq(x, axis, fmt="e4m3"):
    dtype, down = {"e4m3": (ml_dtypes.float8_e4m3fn, 7), "e5m2": (ml_dtypes.float8_e5m2, 14)}[fmt]
    v = np.moveaxis(np.asarray(x, np.float32).astype(ml_dtypes.bfloat16).astype(np.float64), axis, -1)
    blocks = v.reshape(v.shape[:-1] + (-1, 32))
    amax = np.abs(blocks).max(-1, keepdims=True)
    byte = np.maximum(np.where(amax > 0, np.frexp(amax)[1] - 1 + 127, 0) - down, 1)
    scale = np.exp2(byte - 127.0)
    codes = (blocks / scale).astype(np.float32).astype(dtype).astype(np.float64)
    return np.moveaxis((codes * scale).reshape(v.shape), -1, axis)


WIDE = False


def mx_kscale(k):
    if not WIDE:
        return np.ones(k)
    levels = np.array([24, -24, 12, -12, 0])
    if k % 512:
        return np.exp2(np.random.permutation(np.resize(levels, k // 32))).repeat(32)
    a = np.empty((k // 512, 16))
    for p in range(k // 512):
        a[p, :8] = np.random.permutation(np.resize(levels, 8))
        for g in range(8):
            far = levels[np.abs(levels - a[p, g]) >= 10]
            a[p, g + 8] = far[np.random.randint(len(far))]
    return np.exp2(a.ravel()).repeat(32)


def f64(x):
    return np.asarray(x).astype(np.float64)


E2M1 = np.array([0.0, 0.5, 1.0, 1.5, 2.0, 3.0, 4.0, 6.0, -0.0, -0.5, -1.0, -1.5, -2.0, -3.0, -4.0, -6.0])


def pack_weight(w, fmt):
    k, n = w.shape
    w = f64(np.asarray(w, np.float32).astype(ml_dtypes.bfloat16)).reshape(k // 32, 32, n)
    amax = np.abs(w).max(1)
    if fmt == "e4m3":
        byte = np.frexp(amax)[1] - 1 + 127 - 7
    else:
        mant, ex = np.frexp(amax / 6.0)
        byte = np.where(mant > 0.5, ex, ex - 1) + 127
    byte = np.clip(np.where(amax > 0, byte, 1), 1, 254)
    scaled = (w * np.exp2(127.0 - byte)[:, None, :]).reshape(k, n).astype(np.float32)
    by_word = np.ascontiguousarray(scaled.reshape(k // 512, 128, 4, n).transpose(0, 1, 3, 2))
    if fmt == "e4m3":
        words = by_word.astype(ml_dtypes.float8_e4m3fn).view(np.uint8)
    else:
        c = by_word.astype(ml_dtypes.float4_e2m1fn).view(np.uint8) & 0xF
        words = (c[..., 0::2] | (c[..., 1::2] << 4)).reshape(k // 512, 128, 2 * n)
    return np.ascontiguousarray(words), np.ascontiguousarray(byte.astype(np.uint8).reshape(k // 512, 16, n))


def unpack_weight(words, scales, fmt):
    g, _, n = scales.shape
    words = np.ascontiguousarray(words).reshape(g, 128, n, -1)
    if fmt == "e4m3":
        vals = words.view(ml_dtypes.float8_e4m3fn).astype(np.float64)
    else:
        nib = np.empty((g, 128, n, 4), np.uint8)
        nib[..., 0::2] = words & 0xF
        nib[..., 1::2] = words >> 4
        vals = E2M1[nib]
    vals = vals * np.repeat(np.exp2(scales.astype(np.float64) - 127.0), 8, axis=1)[..., None]
    return vals.transpose(0, 1, 3, 2).reshape(g * 512, n)


def planes(y):
    n, m = y.shape
    v = y.astype(np.float32).astype(ml_dtypes.bfloat16).astype(np.float64).reshape(n // 32, 32, m)
    top = np.abs(v).max(1)
    byte = np.clip(np.where(top > 0, np.frexp(top)[1] - 1 + 127 - 7, 1), 1, 254)
    codes = (v * np.exp2(127.0 - byte)[:, None, :]).reshape(n, m).astype(np.float32).astype(ml_dtypes.float8_e4m3fn).view(np.uint8)
    words = codes.reshape(n // 512, 128, 4, m).transpose(0, 1, 3, 2)
    return np.ascontiguousarray(words), np.ascontiguousarray(byte.astype(np.uint8).reshape(n // 512, 16, m))


K, R, N, T = 1536, 512, 512, 1536


def setup_inputs():
    n = np.random.standard_normal
    s = mx_kscale(K)[:, None]
    u = mx_kscale(R)[:, None]
    p_wb = pack_weight(0.7 * n((K, N)) / np.sqrt(K) / s, "e4m3")
    p_dn = pack_weight(n((K, R)) / np.sqrt(K) / s * u.T, "e2m1")
    p_upw = pack_weight(n((R, N)) / np.sqrt(R) / u, "e2m1")
    return {
        "x": (n((K, T)) * s).astype(np.float32),
        "wb_words": p_wb[0],
        "wb_scales": p_wb[1],
        "dn_words": p_dn[0],
        "dn_scales": p_dn[1],
        "upw_words": p_upw[0],
        "upw_scales": p_upw[1],
        "x0": (n((N, T))).astype(np.float32),
        "b": (0.3 * n(N)).astype(np.float32),
        "xr": (n((N, T))).astype(np.float32),
    }


def reference(x, wb_words, wb_scales, dn_words, dn_scales, upw_words, upw_scales, x0, b, xr):
    x_ = mxq(f64(x), 0, "e4m3")
    wb_ = unpack_weight(wb_words, wb_scales, "e4m3")
    dn_ = unpack_weight(dn_words, dn_scales, "e2m1")
    upw_ = unpack_weight(upw_words, upw_scales, "e2m1")
    hs = dn_.T @ x_
    h_ = mxq(hs, 0, "e4m3")
    y = wb_.T @ x_ + upw_.T @ h_
    out_0 = f64(x0) * (y + f64(b)[:, None]) + f64(xr)
    return (out_0,) + planes(out_0)

@@ -1,0 +1,300 @@
+from contextlib import ExitStack
+
+import concourse.mybir as mybir
+
+K, R, N, T = 1536, 512, 512, 1536
+FLOPS = 2 * T * (K * R + K * N + R * N)
+
+F32 = mybir.dt.float32
+BF16 = mybir.dt.bfloat16
+I32 = mybir.dt.int32
+U8 = mybir.dt.uint8
+FP8X4 = mybir.dt.float8_e4m3fn_x4
+FP4X4 = mybir.dt.float4_e2m1fn_x4
+ADD = mybir.AluOpType.add
+MULT = mybir.AluOpType.mult
+
+P = 128
+PACK = 4
+KP = P * PACK
+PASSES = K // KP
+TC = 512
+CHUNKS = T // TC
+HALF = TC // 2
+HN = 128
+
+
+def tile_mix_cross_pl_kernel(
+    tc, x, wb_words, wb_scales, dn_words, dn_scales, upw_words, upw_scales, x0, b, xr, out_0, out_1, out_2
+):
+    nc = tc.nc
+    with ExitStack() as ctx:
+        keep = ctx.enter_context(tc.tile_pool(name="keep", bufs=1))
+        stage = ctx.enter_context(tc.tile_pool(name="stage", bufs=3))
+        hps = ctx.enter_context(tc.psum_pool(name="hps", bufs=1))
+        yps = ctx.enter_context(tc.psum_pool(name="yps", bufs=1))
+        ctx.enter_context(tc.manual_schedule())
+
+        def kept(shape, dtype, name):
+            return keep.tile(shape, dtype, name=name, align_bytes=64)
+
+        x_raw = {(c, a): kept([P, PACK, TC], F32, f"x_raw{c}{a}") for c in range(CHUNKS) for a in range(PASSES)}
+        x0_t = [kept([P, PACK, TC], F32, f"x0_t{c}") for c in range(CHUNKS)]
+        xr_t = [kept([P, PACK, TC], F32, f"xr_t{c}") for c in range(CHUNKS)]
+        b_t = kept([P, PACK], F32, "b_t")
+        wb_raw = kept([P, PASSES, N], I32, "wb_raw")
+        dn_raw = kept([P, PASSES, 2 * R], U8, "dn_raw")
+        up_raw = kept([P, 1, 2 * N], U8, "up_raw")
+        wbs_raw = kept([P, PASSES, N], U8, "wbs_raw")
+        dns_raw = kept([P, PASSES, R], U8, "dns_raw")
+        ups_raw = kept([P, 1, N], U8, "ups_raw")
+        wb_c = kept([P, PASSES, N], I32, "wb_c")
+        dn_c = kept([P, PASSES, 2 * R], U8, "dn_c")
+        up_c = kept([P, 1, 2 * N], U8, "up_c")
+        wb_s = kept([P, PASSES, N], U8, "wb_s")
+        dn_s = kept([P, PASSES, R], U8, "dn_s")
+        up_s = kept([P, 1, N], U8, "up_s")
+        x_c = {(c, a): kept([P, TC], I32, f"x_c{c}{a}") for c in range(CHUNKS) for a in range(PASSES)}
+        x_s = {(c, a): kept([P, TC], U8, f"x_s{c}{a}") for c in range(CHUNKS) for a in range(PASSES)}
+        h_c = [kept([P, TC], I32, f"h_c{c}") for c in range(CHUNKS)]
+        h_s = [kept([P, TC], U8, f"h_s{c}") for c in range(CHUNKS)]
+        o_c = [kept([P, TC], I32, f"o_c{c}") for c in range(CHUNKS)]
+        o_s = kept([P, T], U8, "o_s")
+
+        def cols(c):
+            return slice(c * TC, (c + 1) * TC)
+
+        def rows4(dram, r0, c):
+            return dram[r0 : r0 + KP, cols(c)].rearrange("(p j) t -> p j t", j=PACK)
+
+        def load_x(c, a):
+            nc.sync.dma_start(out=x_raw[c, a][:], in_=rows4(x, a * KP, c))
+
+        def load_scales(dst, src, q):
+            nc.sync.dma_start(
+                out=dst[32 * q : 32 * q + 4].bitcast(I32),
+                in_=src[:, 4 * q : 4 * q + 4, :].rearrange("a r n -> r a n").bitcast(I32),
+            )
+
+        for raw in (dns_raw, wbs_raw, ups_raw):
+            nc.vector.memset(raw[:].bitcast(I32), 0)
+
+        nc.sync.dma_start(out=dn_raw[:].bitcast(I32), in_=dn_words.rearrange("a p n -> p a n").bitcast(I32))
+        load_x(0, 0)
+        load_scales(dns_raw, dn_scales, 0)
+        load_scales(dns_raw, dn_scales, 1)
+        load_x(0, 1)
+        load_scales(dns_raw, dn_scales, 2)
+        load_scales(dns_raw, dn_scales, 3)
+        load_x(0, 2)
+        nc.sync.dma_start(out=wb_raw[:], in_=wb_words.rearrange("a p n i -> p a (n i)").bitcast(I32))
+        load_scales(wbs_raw, wb_scales, 0)
+        load_scales(wbs_raw, wb_scales, 1)
+        load_x(1, 0)
+        load_scales(wbs_raw, wb_scales, 2)
+        load_scales(wbs_raw, wb_scales, 3)
+        nc.sync.dma_start(out=up_raw[:].bitcast(I32), in_=upw_words.rearrange("a p n -> p a n").bitcast(I32))
+        load_scales(ups_raw, upw_scales, 0)
+        load_x(1, 1)
+        load_scales(ups_raw, upw_scales, 1)
+        load_scales(ups_raw, upw_scales, 2)
+        load_scales(ups_raw, upw_scales, 3)
+        nc.sync.dma_start(out=b_t[:], in_=b.rearrange("(p j) -> p j", j=PACK))
+        load_x(1, 2)
+        nc.sync.dma_start(out=x0_t[0][:], in_=rows4(x0, 0, 0))
+        nc.sync.dma_start(out=xr_t[0][:], in_=rows4(xr, 0, 0))
+        for a in range(PASSES):
+            load_x(2, a)
+        for c in (1, 2):
+            nc.sync.dma_start(out=x0_t[c][:], in_=rows4(x0, 0, c))
+            nc.sync.dma_start(out=xr_t[c][:], in_=rows4(xr, 0, c))
+
+        def deal_fp8_words(dst, src, a):
+            nc.vector.tensor_copy(
+                out=dst[:, a, :].rearrange("p (j g m) -> p g j m", j=PACK, m=4),
+                in_=src[:, a, :].rearrange("p (g m j) -> p g j m", j=PACK, m=4),
+            )
+
+        def deal_fp4_words(dst, src, a):
+            nc.vector.tensor_copy(
+                out=dst[:, a, :].rearrange("p (j g m e) -> p g j m e", j=PACK, m=8, e=2),
+                in_=src[:, a, :].rearrange("p (g m j e) -> p g j m e", j=PACK, m=8, e=2),
+            )
+
+        def deal_scales(dst, src):
+            nc.vector.tensor_copy(
+                out=dst[:].rearrange("p a (j g m) -> p a g j m", j=PACK, m=16),
+                in_=src[:].rearrange("p a (g m j) -> p a g j m", j=PACK, m=16),
+            )
+
+        def interleave(copy, dst, src, half):
+            t = slice(half * HALF, (half + 1) * HALF)
+            copy(
+                out=dst[:, t, :].rearrange("p (g i) j -> p g j i", i=4),
+                in_=src[:, :, t].rearrange("p j (g i) -> p g j i", i=4),
+            )
+
+        def quantize(codes, scales, rounded):
+            nc.vector.quantize_mx(
+                out=codes.bitcast(FP8X4), scales=scales, in_=rounded[:].rearrange("p t j -> p (t j)")
+            )
+
+        xb, hb, ob, hbank, ybank = {}, {}, {}, {}, {}
+
+        def round_x(c, a):
+            xb[c, a] = stage.tile([P, TC, PACK], BF16, name="xb", align_bytes=64)
+            interleave(nc.vector.tensor_copy, xb[c, a], x_raw[c, a], 0)
+            interleave(nc.scalar.copy, xb[c, a], x_raw[c, a], 1)
+
+        def quant_x(c, a):
+            quantize(x_c[c, a][:], x_s[c, a][:], xb[c, a])
+
+        def h_pass(c, a):
+            for s in range(TC // HN):
+                if a == 0:
+                    hbank[c, s] = hps.tile([P, PACK, HN], F32, name=f"hbank{s}")
+                t = slice(s * HN, (s + 1) * HN)
+                for j in range(PACK):
+                    nc.tensor.matmul_mx(
+                        out=hbank[c, s][:, j, :],
+                        lhsT=dn_c[:, a, 2 * P * j : 2 * P * (j + 1)].bitcast(FP4X4),
+                        lhsT_scale=dn_s[:, a, P * j : P * (j + 1)],
+                        rhs=x_c[c, a][:, t].bitcast(FP8X4),
+                        rhs_scale=x_s[c, a][:, t],
+                        start=(a == 0 and j == 0),
+                        stop=(a == PASSES - 1 and j == PACK - 1),
+                    )
+
+        def round_h(c):
+            hb[c] = stage.tile([P, TC, PACK], BF16, name="hb", bufs=2, align_bytes=64)
+            for s in range(TC // HN):
+                nc.scalar.copy(
+                    out=hb[c][:, s * HN : (s + 1) * HN, :], in_=hbank[c, s][:].rearrange("p j t -> p t j")
+                )
+
+        def quant_h(c):
+            quantize(h_c[c][:], h_s[c][:], hb[c])
+
+        def y_full(c):
+            for j in range(PACK):
+                ybank[c, j] = yps.tile([P, TC], F32, name=f"ybank{j}")
+                for a in range(PASSES):
+                    nc.tensor.matmul_mx(
+                        out=ybank[c, j][:],
+                        lhsT=wb_c[:, a, P * j : P * (j + 1)].bitcast(FP8X4),
+                        lhsT_scale=wb_s[:, a, P * j : P * (j + 1)],
+                        rhs=x_c[c, a][:].bitcast(FP8X4),
+                        rhs_scale=x_s[c, a][:],
+                        start=(a == 0),
+                        stop=False,
+                    )
+
+        def y_low(c):
+            for j in range(PACK):
+                nc.tensor.matmul_mx(
+                    out=ybank[c, j][:],
+                    lhsT=up_c[:, 0, 2 * P * j : 2 * P * (j + 1)].bitcast(FP4X4),
+                    lhsT_scale=up_s[:, 0, P * j : P * (j + 1)],
+                    rhs=h_c[c][:].bitcast(FP8X4),
+                    rhs_scale=h_s[c][:],
+                    start=False,
+                    stop=True,
+                )
+
+        def scale_y(c):
+            for j in range(PACK):
+                nc.vector.scalar_tensor_tensor(
+                    out=x0_t[c][:, j, :],
+                    in0=ybank[c, j][:],
+                    scalar=b_t[:, j : j + 1],
+                    in1=x0_t[c][:, j, :],
+                    op0=ADD,
+                    op1=MULT,
+                )
+
+        def add_xr(c, half):
+            t = slice(half * HALF, (half + 1) * HALF)
+            nc.vector.tensor_tensor(out=xr_t[c][:, :, t], in0=x0_t[c][:, :, t], in1=xr_t[c][:, :, t], op=ADD)
+
+        def round_out(c, half, copy):
+            if half == 0:
+                ob[c] = stage.tile([P, TC, PACK], BF16, name="ob", bufs=2, align_bytes=64)
+            interleave(copy, ob[c], xr_t[c], half)
+
+        def quant_out(c):
+            quantize(o_c[c][:], o_s[:, cols(c)], ob[c])
+
+        for a in range(PASSES):
+            deal_fp4_words(dn_c, dn_raw, a)
+        round_x(0, 0)
+        quant_x(0, 0)
+        round_x(0, 1)
+        deal_scales(dn_s, dns_raw)
+        quant_x(0, 1)
+        h_pass(0, 0)
+        h_pass(0, 1)
+        round_x(0, 2)
+        quant_x(0, 2)
+        h_pass(0, 2)
+        round_h(0)
+        for a in range(PASSES):
+            deal_fp8_words(wb_c, wb_raw, a)
+        round_x(1, 0)
+        deal_scales(wb_s, wbs_raw)
+        quant_h(0)
+        quant_x(1, 0)
+        y_full(0)
+        h_pass(1, 0)
+        deal_fp4_words(up_c, up_raw, 0)
+        round_x(1, 1)
+        deal_scales(up_s, ups_raw)
+        quant_x(1, 1)
+        h_pass(1, 1)
+        y_low(0)
+        round_x(1, 2)
+        quant_x(1, 2)
+        h_pass(1, 2)
+        round_h(1)
+        scale_y(0)
+        y_full(1)
+        quant_h(1)
+        y_low(1)
+        add_xr(0, 0)
+        add_xr(0, 1)
+        round_x(2, 0)
+        quant_x(2, 0)
+        h_pass(2, 0)
+        round_out(0, 0, nc.scalar.copy)
+        round_x(2, 1)
+        quant_x(2, 1)
+        h_pass(2, 1)
+        round_out(0, 1, nc.scalar.copy)
+        round_x(2, 2)
+        quant_out(0)
+        quant_x(2, 2)
+        h_pass(2, 2)
+        round_h(2)
+        scale_y(1)
+        y_full(2)
+        add_xr(1, 0)
+        quant_h(2)
+        y_low(2)
+        add_xr(1, 1)
+        round_out(1, 0, nc.scalar.copy)
+        round_out(1, 1, nc.scalar.copy)
+        scale_y(2)
+        quant_out(1)
+        add_xr(2, 0)
+        add_xr(2, 1)
+        round_out(2, 0, nc.scalar.copy)
+        round_out(2, 1, nc.vector.tensor_copy)
+        quant_out(2)
+
+        words_out = out_1[0].rearrange("p t j -> p (t j)").bitcast(I32)
+        for c in range(CHUNKS):
+            nc.sync.dma_start(out=rows4(out_0, 0, c), in_=xr_t[c][:])
+            nc.sync.dma_start(out=words_out[:, cols(c)], in_=o_c[c][:])
+        for q in range(4):
+            nc.sync.dma_start(
+                out=out_2[0, 4 * q : 4 * q + 4, :].bitcast(I32), in_=o_s[32 * q : 32 * q + 4, :].bitcast(I32)
+            )

@@ -76,38 +76,55 @@ def tile_mix_cross_pl_kernel(
                 in_=src[:, 4 * q : 4 * q + 4, :].rearrange("a r n -> r a n").bitcast(I32),
             )
 
+        def load_rows(dst, src, c):
+            nc.sync.dma_start(out=dst[c][:], in_=rows4(src, 0, c))
+
+        def load_dn():
+            nc.sync.dma_start(out=dn_raw[:].bitcast(I32), in_=dn_words.rearrange("a p n -> p a n").bitcast(I32))
+
+        def load_wb():
+            nc.sync.dma_start(out=wb_raw[:], in_=wb_words.rearrange("a p n i -> p a (n i)").bitcast(I32))
+
+        def load_up():
+            nc.sync.dma_start(out=up_raw[:].bitcast(I32), in_=upw_words.rearrange("a p n -> p a n").bitcast(I32))
+
+        def load_b():
+            nc.sync.dma_start(out=b_t[:], in_=b.rearrange("(p j) -> p j", j=PACK))
+
         for raw in (dns_raw, wbs_raw, ups_raw):
             nc.vector.memset(raw[:].bitcast(I32), 0)
 
-        nc.sync.dma_start(out=dn_raw[:].bitcast(I32), in_=dn_words.rearrange("a p n -> p a n").bitcast(I32))
-        load_x(0, 0)
         load_scales(dns_raw, dn_scales, 0)
         load_scales(dns_raw, dn_scales, 1)
-        load_x(0, 1)
         load_scales(dns_raw, dn_scales, 2)
         load_scales(dns_raw, dn_scales, 3)
+        load_dn()
+        load_x(0, 0)
+        load_x(0, 1)
         load_x(0, 2)
-        nc.sync.dma_start(out=wb_raw[:], in_=wb_words.rearrange("a p n i -> p a (n i)").bitcast(I32))
         load_scales(wbs_raw, wb_scales, 0)
         load_scales(wbs_raw, wb_scales, 1)
-        load_x(1, 0)
         load_scales(wbs_raw, wb_scales, 2)
         load_scales(wbs_raw, wb_scales, 3)
-        nc.sync.dma_start(out=up_raw[:].bitcast(I32), in_=upw_words.rearrange("a p n -> p a n").bitcast(I32))
+        load_wb()
+        load_x(1, 0)
+        load_up()
         load_scales(ups_raw, upw_scales, 0)
         load_x(1, 1)
         load_scales(ups_raw, upw_scales, 1)
         load_scales(ups_raw, upw_scales, 2)
         load_scales(ups_raw, upw_scales, 3)
-        nc.sync.dma_start(out=b_t[:], in_=b.rearrange("(p j) -> p j", j=PACK))
+        load_b()
         load_x(1, 2)
-        nc.sync.dma_start(out=x0_t[0][:], in_=rows4(x0, 0, 0))
-        nc.sync.dma_start(out=xr_t[0][:], in_=rows4(xr, 0, 0))
-        for a in range(PASSES):
-            load_x(2, a)
-        for c in (1, 2):
-            nc.sync.dma_start(out=x0_t[c][:], in_=rows4(x0, 0, c))
-            nc.sync.dma_start(out=xr_t[c][:], in_=rows4(xr, 0, c))
+        load_rows(x0_t, x0, 0)
+        load_rows(xr_t, xr, 0)
+        load_x(2, 0)
+        load_x(2, 1)
+        load_x(2, 2)
+        load_rows(x0_t, x0, 1)
+        load_rows(xr_t, xr, 1)
+        load_rows(x0_t, x0, 2)
+        load_rows(xr_t, xr, 2)
 
         def deal_fp8_words(dst, src, a):
             nc.vector.tensor_copy(
@@ -127,8 +144,7 @@ def tile_mix_cross_pl_kernel(
                 in_=src[:].rearrange("p a (g m j) -> p a g j m", j=PACK, m=16),
             )
 
-        def interleave(copy, dst, src, half):
-            t = slice(half * HALF, (half + 1) * HALF)
+        def interleave(copy, dst, src, t):
             copy(
                 out=dst[:, t, :].rearrange("p (g i) j -> p g j i", i=4),
                 in_=src[:, :, t].rearrange("p j (g i) -> p g j i", i=4),
@@ -141,10 +157,12 @@ def tile_mix_cross_pl_kernel(
 
         xb, hb, ob, hbank, ybank = {}, {}, {}, {}, {}
 
-        def round_x(c, a):
+        def round_x(c, a, split):
             xb[c, a] = stage.tile([P, TC, PACK], BF16, name="xb", align_bytes=64)
-            interleave(nc.vector.tensor_copy, xb[c, a], x_raw[c, a], 0)
-            interleave(nc.scalar.copy, xb[c, a], x_raw[c, a], 1)
+            if split:
+                interleave(nc.vector.tensor_copy, xb[c, a], x_raw[c, a], slice(0, split))
+            if split < TC:
+                interleave(nc.scalar.copy, xb[c, a], x_raw[c, a], slice(split, TC))
 
         def quant_x(c, a):
             quantize(x_c[c, a][:], x_s[c, a][:], xb[c, a])
@@ -165,10 +183,11 @@ def tile_mix_cross_pl_kernel(
                         stop=(a == PASSES - 1 and j == PACK - 1),
                     )
 
-        def round_h(c):
+        def round_h(c, on_vector=()):
             hb[c] = stage.tile([P, TC, PACK], BF16, name="hb", bufs=2, align_bytes=64)
             for s in range(TC // HN):
-                nc.scalar.copy(
+                copy = nc.vector.tensor_copy if s in on_vector else nc.scalar.copy
+                copy(
                     out=hb[c][:, s * HN : (s + 1) * HN, :], in_=hbank[c, s][:].rearrange("p j t -> p t j")
                 )
 
@@ -188,6 +207,28 @@ def tile_mix_cross_pl_kernel(
                         start=(a == 0),
                         stop=False,
                     )
+
+        def y_pass(c, a):
+            for j in range(PACK):
+                if a == 0:
+                    ybank[c, j] = yps.tile([P, TC], F32, name=f"ybank{j}")
+                nc.tensor.matmul_mx(
+                    out=ybank[c, j][:],
+                    lhsT=wb_c[:, a, P * j : P * (j + 1)].bitcast(FP8X4),
+                    lhsT_scale=wb_s[:, a, P * j : P * (j + 1)],
+                    rhs=x_c[c, a][:].bitcast(FP8X4),
+                    rhs_scale=x_s[c, a][:],
+                    start=(a == 0),
+                    stop=False,
+                )
+
+        def quantize_half(codes, scales, rounded, half):
+            t = slice(half * HALF, (half + 1) * HALF)
+            nc.vector.quantize_mx(
+                out=codes[:, t].bitcast(FP8X4),
+                scales=scales[:, t],
+                in_=rounded[:, t, :].rearrange("p t j -> p (t j)"),
+            )
 
         def y_low(c):
             for j in range(PACK):
@@ -212,88 +253,124 @@ def tile_mix_cross_pl_kernel(
                     op1=MULT,
                 )
 
+        def scale_pair(c, u):
+            for j in (2 * u, 2 * u + 1):
+                nc.vector.scalar_tensor_tensor(
+                    out=x0_t[c][:, j, :],
+                    in0=ybank[c, j][:],
+                    scalar=b_t[:, j : j + 1],
+                    in1=x0_t[c][:, j, :],
+                    op0=ADD,
+                    op1=MULT,
+                )
+
+        def add_pair(c, u):
+            js = slice(2 * u, 2 * u + 2)
+            nc.vector.tensor_tensor(out=xr_t[c][:, js, :], in0=x0_t[c][:, js, :], in1=xr_t[c][:, js, :], op=ADD)
+
+        def round_out_split(c, split):
+            ob[c] = stage.tile([P, TC, PACK], BF16, name="ob", bufs=3, align_bytes=64)
+            interleave(nc.scalar.copy, ob[c], xr_t[c], slice(split, TC))
+            if split:
+                interleave(nc.vector.tensor_copy, ob[c], xr_t[c], slice(0, split))
+
         def add_xr(c, half):
             t = slice(half * HALF, (half + 1) * HALF)
             nc.vector.tensor_tensor(out=xr_t[c][:, :, t], in0=x0_t[c][:, :, t], in1=xr_t[c][:, :, t], op=ADD)
 
         def round_out(c, half, copy):
             if half == 0:
-                ob[c] = stage.tile([P, TC, PACK], BF16, name="ob", bufs=2, align_bytes=64)
-            interleave(copy, ob[c], xr_t[c], half)
+                ob[c] = stage.tile([P, TC, PACK], BF16, name="ob", bufs=3, align_bytes=64)
+            interleave(copy, ob[c], xr_t[c], slice(half * HALF, (half + 1) * HALF))
 
         def quant_out(c):
             quantize(o_c[c][:], o_s[:, cols(c)], ob[c])
 
-        for a in range(PASSES):
-            deal_fp4_words(dn_c, dn_raw, a)
-        round_x(0, 0)
-        quant_x(0, 0)
-        round_x(0, 1)
         deal_scales(dn_s, dns_raw)
-        quant_x(0, 1)
-        h_pass(0, 0)
-        h_pass(0, 1)
-        round_x(0, 2)
-        quant_x(0, 2)
-        h_pass(0, 2)
+        deal_fp4_words(dn_c, dn_raw, 0)
+        deal_fp4_words(dn_c, dn_raw, 1)
+        deal_fp4_words(dn_c, dn_raw, 2)
+        round_x(0,0,0)
+        quant_x(0,0)
+        h_pass(0,0)
+        round_x(0,1,256)
+        quant_x(0,1)
+        h_pass(0,1)
+        round_x(0,2,256)
+        quant_x(0,2)
+        h_pass(0,2)
         round_h(0)
-        for a in range(PASSES):
-            deal_fp8_words(wb_c, wb_raw, a)
-        round_x(1, 0)
         deal_scales(wb_s, wbs_raw)
-        quant_h(0)
-        quant_x(1, 0)
+        deal_fp8_words(wb_c, wb_raw, 0)
+        deal_fp8_words(wb_c, wb_raw, 1)
+        deal_fp8_words(wb_c, wb_raw, 2)
         y_full(0)
-        h_pass(1, 0)
+        round_x(1,0,384)
+        quant_h(0)
+        quant_x(1,0)
+        h_pass(1,0)
         deal_fp4_words(up_c, up_raw, 0)
-        round_x(1, 1)
+        round_x(1,1,0)
         deal_scales(up_s, ups_raw)
-        quant_x(1, 1)
-        h_pass(1, 1)
         y_low(0)
-        round_x(1, 2)
-        quant_x(1, 2)
-        h_pass(1, 2)
+        quant_x(1,1)
+        h_pass(1,1)
+        round_x(1,2,256)
+        quant_x(1,2)
+        h_pass(1,2)
         round_h(1)
         scale_y(0)
         y_full(1)
+        add_pair(0,0)
         quant_h(1)
         y_low(1)
-        add_xr(0, 0)
-        add_xr(0, 1)
-        round_x(2, 0)
-        quant_x(2, 0)
-        h_pass(2, 0)
-        round_out(0, 0, nc.scalar.copy)
-        round_x(2, 1)
-        quant_x(2, 1)
-        h_pass(2, 1)
-        round_out(0, 1, nc.scalar.copy)
-        round_x(2, 2)
+        add_pair(0,1)
+        round_x(2,0,256)
+        quant_x(2,0)
+        h_pass(2,0)
+        round_out(0,0,nc.scalar.copy)
+        round_x(2,1,256)
+        quant_x(2,1)
+        h_pass(2,1)
+        round_out(0,1,nc.scalar.copy)
+        round_x(2,2,256)
         quant_out(0)
-        quant_x(2, 2)
-        h_pass(2, 2)
+        quant_x(2,2)
+        h_pass(2,2)
         round_h(2)
         scale_y(1)
         y_full(2)
-        add_xr(1, 0)
+        add_pair(1,0)
         quant_h(2)
         y_low(2)
-        add_xr(1, 1)
-        round_out(1, 0, nc.scalar.copy)
-        round_out(1, 1, nc.scalar.copy)
-        scale_y(2)
+        add_pair(1,1)
+        round_out_split(1,0)
+        scale_pair(2,0)
+        add_pair(2,0)
+        scale_pair(2,1)
         quant_out(1)
-        add_xr(2, 0)
-        add_xr(2, 1)
-        round_out(2, 0, nc.scalar.copy)
-        round_out(2, 1, nc.vector.tensor_copy)
+        add_pair(2,1)
+        round_out_split(2,320)
         quant_out(2)
 
         words_out = out_1[0].rearrange("p t j -> p (t j)").bitcast(I32)
-        for c in range(CHUNKS):
+
+        def store_out(c):
             nc.sync.dma_start(out=rows4(out_0, 0, c), in_=xr_t[c][:])
+
+        def store_pair(c, u):
+            nc.sync.dma_start(out=rows4(out_0, 0, c)[:, 2 * u : 2 * u + 2, :], in_=xr_t[c][:, 2 * u : 2 * u + 2, :])
+
+        def store_words(c):
             nc.sync.dma_start(out=words_out[:, cols(c)], in_=o_c[c][:])
+
+        store_out(0)
+        store_words(0)
+        store_out(1)
+        store_pair(2,0)
+        store_words(1)
+        store_pair(2,1)
+        store_words(2)
         for q in range(4):
             nc.sync.dma_start(
                 out=out_2[0, 4 * q : 4 * q + 4, :].bitcast(I32), in_=o_s[32 * q : 32 * q + 4, :].bitcast(I32)

@@ -71,7 +71,8 @@ def tile_mix_cross_pl_kernel(
             nc.sync.dma_start(out=x_raw[c, a][:], in_=rows4(x, a * KP, c))
 
         def load_scales(dst, src, q):
-            nc.sync.dma_start(
+            queue = nc.sync if dst is dns_raw else nc.gpsimd
+            queue.dma_start(
                 out=dst[32 * q : 32 * q + 4].bitcast(I32),
                 in_=src[:, 4 * q : 4 * q + 4, :].rearrange("a r n -> r a n").bitcast(I32),
             )
@@ -89,32 +90,32 @@ def tile_mix_cross_pl_kernel(
             nc.sync.dma_start(out=up_raw[:].bitcast(I32), in_=upw_words.rearrange("a p n -> p a n").bitcast(I32))
 
         def load_b():
-            nc.sync.dma_start(out=b_t[:], in_=b.rearrange("(p j) -> p j", j=PACK))
+            nc.gpsimd.dma_start(out=b_t[:], in_=b.rearrange("(p j) -> p j", j=PACK))
 
-        for raw in (dns_raw, wbs_raw, ups_raw):
+        for raw in (wbs_raw, dns_raw, ups_raw):
             nc.vector.memset(raw[:].bitcast(I32), 0)
 
+        load_dn()
         load_scales(dns_raw, dn_scales, 0)
         load_scales(dns_raw, dn_scales, 1)
         load_scales(dns_raw, dn_scales, 2)
         load_scales(dns_raw, dn_scales, 3)
-        load_dn()
-        load_x(0, 0)
-        load_x(0, 1)
-        load_x(0, 2)
         load_scales(wbs_raw, wb_scales, 0)
         load_scales(wbs_raw, wb_scales, 1)
         load_scales(wbs_raw, wb_scales, 2)
         load_scales(wbs_raw, wb_scales, 3)
-        load_wb()
-        load_x(1, 0)
-        load_up()
         load_scales(ups_raw, upw_scales, 0)
-        load_x(1, 1)
         load_scales(ups_raw, upw_scales, 1)
         load_scales(ups_raw, upw_scales, 2)
         load_scales(ups_raw, upw_scales, 3)
         load_b()
+        load_x(0, 0)
+        load_x(0, 1)
+        load_x(0, 2)
+        load_wb()
+        load_x(1, 0)
+        load_up()
+        load_x(1, 1)
         load_x(1, 2)
         load_rows(x0_t, x0, 0)
         load_rows(xr_t, xr, 0)
@@ -286,8 +287,8 @@ def tile_mix_cross_pl_kernel(
         def quant_out(c):
             quantize(o_c[c][:], o_s[:, cols(c)], ob[c])
 
-        deal_scales(dn_s, dns_raw)
         deal_fp4_words(dn_c, dn_raw, 0)
+        deal_scales(dn_s, dns_raw)
         deal_fp4_words(dn_c, dn_raw, 1)
         deal_fp4_words(dn_c, dn_raw, 2)
         round_x(0,0,0)
@@ -333,9 +334,9 @@ def tile_mix_cross_pl_kernel(
         quant_x(2,1)
         h_pass(2,1)
         round_out(0,1,nc.scalar.copy)
-        round_x(2,2,256)
-        quant_out(0)
+        round_x(2,2,384)
         quant_x(2,2)
+        quant_out(0)
         h_pass(2,2)
         round_h(2)
         scale_y(1)
@@ -372,6 +373,6 @@ def tile_mix_cross_pl_kernel(
         store_pair(2,1)
         store_words(2)
         for q in range(4):
-            nc.sync.dma_start(
+            nc.scalar.dma_start(
                 out=out_2[0, 4 * q : 4 * q + 4, :].bitcast(I32), in_=o_s[32 * q : 32 * q + 4, :].bitcast(I32)
             )

@@ -8,6 +8,7 @@ FLOPS = 2 * T * (K * R + K * N + R * N)
 F32 = mybir.dt.float32
 BF16 = mybir.dt.bfloat16
 I32 = mybir.dt.int32
+U16 = mybir.dt.uint16
 U8 = mybir.dt.uint8
 FP8X4 = mybir.dt.float8_e4m3fn_x4
 FP4X4 = mybir.dt.float4_e2m1fn_x4
@@ -20,7 +21,6 @@ KP = P * PACK
 PASSES = K // KP
 TC = 512
 CHUNKS = T // TC
-HALF = TC // 2
 HN = 128
 
 
@@ -31,54 +31,58 @@ def tile_mix_cross_pl_kernel(
     with ExitStack() as ctx:
         keep = ctx.enter_context(tc.tile_pool(name="keep", bufs=1))
         stage = ctx.enter_context(tc.tile_pool(name="stage", bufs=3))
-        hps = ctx.enter_context(tc.psum_pool(name="hps", bufs=1))
-        yps = ctx.enter_context(tc.psum_pool(name="yps", bufs=1))
+        psum = ctx.enter_context(tc.psum_pool(name="psum", bufs=1))
         ctx.enter_context(tc.manual_schedule())
 
         def kept(shape, dtype, name):
             return keep.tile(shape, dtype, name=name, align_bytes=64)
 
         x_raw = {(c, a): kept([P, PACK, TC], F32, f"x_raw{c}{a}") for c in range(CHUNKS) for a in range(PASSES)}
-        x0_t = [kept([P, PACK, TC], F32, f"x0_t{c}") for c in range(CHUNKS)]
-        xr_t = [kept([P, PACK, TC], F32, f"xr_t{c}") for c in range(CHUNKS)]
+        x0_t = kept([P, PACK, T], F32, "x0_t")
+        xr_t = kept([P, PACK, T], F32, "xr_t")
         b_t = kept([P, PACK], F32, "b_t")
         wb_raw = kept([P, PASSES, N], I32, "wb_raw")
         dn_raw = kept([P, PASSES, 2 * R], U8, "dn_raw")
         up_raw = kept([P, 1, 2 * N], U8, "up_raw")
-        wbs_raw = kept([P, PASSES, N], U8, "wbs_raw")
+        wbs_raw = kept([P, 1, N], U8, "wbs_raw")
         dns_raw = kept([P, PASSES, R], U8, "dns_raw")
         ups_raw = kept([P, 1, N], U8, "ups_raw")
         wb_c = kept([P, PASSES, N], I32, "wb_c")
         dn_c = kept([P, PASSES, 2 * R], U8, "dn_c")
         up_c = kept([P, 1, 2 * N], U8, "up_c")
-        wb_s = kept([P, PASSES, N], U8, "wb_s")
+        wb_s = kept([P, 1, N], U8, "wb_s")
         dn_s = kept([P, PASSES, R], U8, "dn_s")
         up_s = kept([P, 1, N], U8, "up_s")
         x_c = {(c, a): kept([P, TC], I32, f"x_c{c}{a}") for c in range(CHUNKS) for a in range(PASSES)}
         x_s = {(c, a): kept([P, TC], U8, f"x_s{c}{a}") for c in range(CHUNKS) for a in range(PASSES)}
         h_c = [kept([P, TC], I32, f"h_c{c}") for c in range(CHUNKS)]
         h_s = [kept([P, TC], U8, f"h_s{c}") for c in range(CHUNKS)]
-        o_c = [kept([P, TC], I32, f"o_c{c}") for c in range(CHUNKS)]
+        o_c = kept([P, T], I32, "o_c")
         o_s = kept([P, T], U8, "o_s")
 
         def cols(c):
             return slice(c * TC, (c + 1) * TC)
 
-        def rows4(dram, r0, c):
-            return dram[r0 : r0 + KP, cols(c)].rearrange("(p j) t -> p j t", j=PACK)
+        def rows4(dram):
+            return dram.rearrange("(p j) t -> p j t", j=PACK)
 
         def load_x(c, a):
-            nc.sync.dma_start(out=x_raw[c, a][:], in_=rows4(x, a * KP, c))
+            nc.sync.dma_start(out=x_raw[c, a][:], in_=rows4(x[a * KP : (a + 1) * KP, cols(c)]))
 
-        def load_scales(dst, src, q):
-            queue = nc.sync if dst is dns_raw else nc.gpsimd
+        def load_scales(queue, dst, src, q):
             queue.dma_start(
                 out=dst[32 * q : 32 * q + 4].bitcast(I32),
                 in_=src[:, 4 * q : 4 * q + 4, :].rearrange("a r n -> r a n").bitcast(I32),
             )
 
-        def load_rows(dst, src, c):
-            nc.sync.dma_start(out=dst[c][:], in_=rows4(src, 0, c))
+        def load_packed_scales(queue, dst, src, q):
+            queue.dma_start(
+                out=dst[32 * q : 32 * q + 4 * PASSES, 0, :].bitcast(I32),
+                in_=src[:, 4 * q : 4 * q + 4, :].bitcast(I32),
+            )
+
+        def load_slots(dst, src, j0, j1):
+            nc.sync.dma_start(out=dst[:, j0:j1, :], in_=rows4(src)[:, j0:j1, :])
 
         def load_dn():
             nc.sync.dma_start(out=dn_raw[:].bitcast(I32), in_=dn_words.rearrange("a p n -> p a n").bitcast(I32))
@@ -89,44 +93,6 @@ def tile_mix_cross_pl_kernel(
         def load_up():
             nc.sync.dma_start(out=up_raw[:].bitcast(I32), in_=upw_words.rearrange("a p n -> p a n").bitcast(I32))
 
-        def load_b():
-            nc.gpsimd.dma_start(out=b_t[:], in_=b.rearrange("(p j) -> p j", j=PACK))
-
-        for raw in (wbs_raw, dns_raw, ups_raw):
-            nc.vector.memset(raw[:].bitcast(I32), 0)
-
-        load_dn()
-        load_scales(dns_raw, dn_scales, 0)
-        load_scales(dns_raw, dn_scales, 1)
-        load_scales(dns_raw, dn_scales, 2)
-        load_scales(dns_raw, dn_scales, 3)
-        load_scales(wbs_raw, wb_scales, 0)
-        load_scales(wbs_raw, wb_scales, 1)
-        load_scales(wbs_raw, wb_scales, 2)
-        load_scales(wbs_raw, wb_scales, 3)
-        load_scales(ups_raw, upw_scales, 0)
-        load_scales(ups_raw, upw_scales, 1)
-        load_scales(ups_raw, upw_scales, 2)
-        load_scales(ups_raw, upw_scales, 3)
-        load_b()
-        load_x(0, 0)
-        load_x(0, 1)
-        load_x(0, 2)
-        load_wb()
-        load_x(1, 0)
-        load_up()
-        load_x(1, 1)
-        load_x(1, 2)
-        load_rows(x0_t, x0, 0)
-        load_rows(xr_t, xr, 0)
-        load_x(2, 0)
-        load_x(2, 1)
-        load_x(2, 2)
-        load_rows(x0_t, x0, 1)
-        load_rows(xr_t, xr, 1)
-        load_rows(x0_t, x0, 2)
-        load_rows(xr_t, xr, 2)
-
         def deal_fp8_words(dst, src, a):
             nc.vector.tensor_copy(
                 out=dst[:, a, :].rearrange("p (j g m) -> p g j m", j=PACK, m=4),
@@ -135,20 +101,20 @@ def tile_mix_cross_pl_kernel(
 
         def deal_fp4_words(dst, src, a):
             nc.vector.tensor_copy(
-                out=dst[:, a, :].rearrange("p (j g m e) -> p g j m e", j=PACK, m=8, e=2),
-                in_=src[:, a, :].rearrange("p (g m j e) -> p g j m e", j=PACK, m=8, e=2),
+                out=dst[:, a, :].bitcast(U16).rearrange("p (j g m) -> p g j m", j=PACK, m=8),
+                in_=src[:, a, :].bitcast(U16).rearrange("p (g m j) -> p g j m", j=PACK, m=8),
             )
 
-        def deal_scales(dst, src):
+        def deal_scales(dst, src, a):
             nc.vector.tensor_copy(
-                out=dst[:].rearrange("p a (j g m) -> p a g j m", j=PACK, m=16),
-                in_=src[:].rearrange("p a (g m j) -> p a g j m", j=PACK, m=16),
+                out=dst[:, a, :].rearrange("p (j g m) -> p g j m", j=PACK, m=16),
+                in_=src[:, a, :].rearrange("p (g m j) -> p g j m", j=PACK, m=16),
             )
 
-        def interleave(copy, dst, src, t):
+        def interleave(copy, dst, src, t0, t1, base):
             copy(
-                out=dst[:, t, :].rearrange("p (g i) j -> p g j i", i=4),
-                in_=src[:, :, t].rearrange("p j (g i) -> p g j i", i=4),
+                out=dst[:, t0:t1, :].rearrange("p (g i) j -> p g j i", i=4),
+                in_=src[:, :, base + t0 : base + t1].rearrange("p j (g i) -> p g j i", i=4),
             )
 
         def quantize(codes, scales, rounded):
@@ -160,18 +126,18 @@ def tile_mix_cross_pl_kernel(
 
         def round_x(c, a, split):
             xb[c, a] = stage.tile([P, TC, PACK], BF16, name="xb", align_bytes=64)
-            if split:
-                interleave(nc.vector.tensor_copy, xb[c, a], x_raw[c, a], slice(0, split))
             if split < TC:
-                interleave(nc.scalar.copy, xb[c, a], x_raw[c, a], slice(split, TC))
+                interleave(nc.scalar.copy, xb[c, a], x_raw[c, a], split, TC, 0)
+            if split:
+                interleave(nc.vector.tensor_copy, xb[c, a], x_raw[c, a], 0, split, 0)
 
         def quant_x(c, a):
             quantize(x_c[c, a][:], x_s[c, a][:], xb[c, a])
 
-        def h_pass(c, a):
+        def h_pass(c, a, bank0=0):
             for s in range(TC // HN):
                 if a == 0:
-                    hbank[c, s] = hps.tile([P, PACK, HN], F32, name=f"hbank{s}")
+                    hbank[c, s] = psum.tile([P, PACK, HN], F32, name=f"bank{bank0 + s}")
                 t = slice(s * HN, (s + 1) * HN)
                 for j in range(PACK):
                     nc.tensor.matmul_mx(
@@ -195,184 +161,195 @@ def tile_mix_cross_pl_kernel(
         def quant_h(c):
             quantize(h_c[c][:], h_s[c][:], hb[c])
 
-        def y_full(c):
-            for j in range(PACK):
-                ybank[c, j] = yps.tile([P, TC], F32, name=f"ybank{j}")
-                for a in range(PASSES):
-                    nc.tensor.matmul_mx(
-                        out=ybank[c, j][:],
-                        lhsT=wb_c[:, a, P * j : P * (j + 1)].bitcast(FP8X4),
-                        lhsT_scale=wb_s[:, a, P * j : P * (j + 1)],
-                        rhs=x_c[c, a][:].bitcast(FP8X4),
-                        rhs_scale=x_s[c, a][:],
-                        start=(a == 0),
-                        stop=False,
-                    )
-
-        def y_pass(c, a):
-            for j in range(PACK):
-                if a == 0:
-                    ybank[c, j] = yps.tile([P, TC], F32, name=f"ybank{j}")
+        def y_base(c, j, bank):
+            ybank[c, j] = psum.tile([P, TC], F32, name=f"bank{bank}")
+            for a in range(PASSES):
                 nc.tensor.matmul_mx(
                     out=ybank[c, j][:],
                     lhsT=wb_c[:, a, P * j : P * (j + 1)].bitcast(FP8X4),
-                    lhsT_scale=wb_s[:, a, P * j : P * (j + 1)],
+                    lhsT_scale=wb_s[4 * a :, 0, P * j : P * (j + 1)],
                     rhs=x_c[c, a][:].bitcast(FP8X4),
                     rhs_scale=x_s[c, a][:],
                     start=(a == 0),
                     stop=False,
                 )
 
-        def quantize_half(codes, scales, rounded, half):
-            t = slice(half * HALF, (half + 1) * HALF)
-            nc.vector.quantize_mx(
-                out=codes[:, t].bitcast(FP8X4),
-                scales=scales[:, t],
-                in_=rounded[:, t, :].rearrange("p t j -> p (t j)"),
+        def y_low(c, j):
+            nc.tensor.matmul_mx(
+                out=ybank[c, j][:],
+                lhsT=up_c[:, 0, 2 * P * j : 2 * P * (j + 1)].bitcast(FP4X4),
+                lhsT_scale=up_s[:, 0, P * j : P * (j + 1)],
+                rhs=h_c[c][:].bitcast(FP8X4),
+                rhs_scale=h_s[c][:],
+                start=False,
+                stop=True,
             )
 
-        def y_low(c):
-            for j in range(PACK):
-                nc.tensor.matmul_mx(
-                    out=ybank[c, j][:],
-                    lhsT=up_c[:, 0, 2 * P * j : 2 * P * (j + 1)].bitcast(FP4X4),
-                    lhsT_scale=up_s[:, 0, P * j : P * (j + 1)],
-                    rhs=h_c[c][:].bitcast(FP8X4),
-                    rhs_scale=h_s[c][:],
-                    start=False,
-                    stop=True,
-                )
+        def y_all(c, j, bank):
+            y_base(c, j, bank)
+            y_low(c, j)
 
-        def scale_y(c):
-            for j in range(PACK):
-                nc.vector.scalar_tensor_tensor(
-                    out=x0_t[c][:, j, :],
-                    in0=ybank[c, j][:],
-                    scalar=b_t[:, j : j + 1],
-                    in1=x0_t[c][:, j, :],
-                    op0=ADD,
-                    op1=MULT,
-                )
+        def scale_y(c, j):
+            nc.vector.scalar_tensor_tensor(
+                out=x0_t[:, j, cols(c)],
+                in0=ybank[c, j][:],
+                scalar=b_t[:, j : j + 1],
+                in1=x0_t[:, j, cols(c)],
+                op0=ADD,
+                op1=MULT,
+            )
 
-        def scale_pair(c, u):
-            for j in (2 * u, 2 * u + 1):
-                nc.vector.scalar_tensor_tensor(
-                    out=x0_t[c][:, j, :],
-                    in0=ybank[c, j][:],
-                    scalar=b_t[:, j : j + 1],
-                    in1=x0_t[c][:, j, :],
-                    op0=ADD,
-                    op1=MULT,
-                )
+        def add_xr(j, c0, c1):
+            t = slice(c0 * TC, c1 * TC)
+            nc.vector.tensor_tensor(out=xr_t[:, j, t], in0=x0_t[:, j, t], in1=xr_t[:, j, t], op=ADD)
 
-        def add_pair(c, u):
-            js = slice(2 * u, 2 * u + 2)
-            nc.vector.tensor_tensor(out=xr_t[c][:, js, :], in0=x0_t[c][:, js, :], in1=xr_t[c][:, js, :], op=ADD)
-
-        def round_out_split(c, split):
+        def round_out(c, split):
             ob[c] = stage.tile([P, TC, PACK], BF16, name="ob", bufs=3, align_bytes=64)
-            interleave(nc.scalar.copy, ob[c], xr_t[c], slice(split, TC))
+            if split < TC:
+                interleave(nc.scalar.copy, ob[c], xr_t, split, TC, c * TC)
             if split:
-                interleave(nc.vector.tensor_copy, ob[c], xr_t[c], slice(0, split))
+                interleave(nc.vector.tensor_copy, ob[c], xr_t, 0, split, c * TC)
 
-        def add_xr(c, half):
-            t = slice(half * HALF, (half + 1) * HALF)
-            nc.vector.tensor_tensor(out=xr_t[c][:, :, t], in0=x0_t[c][:, :, t], in1=xr_t[c][:, :, t], op=ADD)
-
-        def round_out(c, half, copy):
-            if half == 0:
+        def round_pair(copy, c, u, t0, t1):
+            if c not in ob:
                 ob[c] = stage.tile([P, TC, PACK], BF16, name="ob", bufs=3, align_bytes=64)
-            interleave(copy, ob[c], xr_t[c], slice(half * HALF, (half + 1) * HALF))
+            js = slice(2 * u, 2 * u + 2)
+            copy(
+                out=ob[c][:, t0:t1, js].rearrange("p (g i) j -> p g j i", i=4),
+                in_=xr_t[:, js, c * TC + t0 : c * TC + t1].rearrange("p j (g i) -> p g j i", i=4),
+            )
 
         def quant_out(c):
-            quantize(o_c[c][:], o_s[:, cols(c)], ob[c])
-
-        deal_fp4_words(dn_c, dn_raw, 0)
-        deal_scales(dn_s, dns_raw)
-        deal_fp4_words(dn_c, dn_raw, 1)
-        deal_fp4_words(dn_c, dn_raw, 2)
-        round_x(0,0,0)
-        quant_x(0,0)
-        h_pass(0,0)
-        round_x(0,1,256)
-        quant_x(0,1)
-        h_pass(0,1)
-        round_x(0,2,256)
-        quant_x(0,2)
-        h_pass(0,2)
-        round_h(0)
-        deal_scales(wb_s, wbs_raw)
-        deal_fp8_words(wb_c, wb_raw, 0)
-        deal_fp8_words(wb_c, wb_raw, 1)
-        deal_fp8_words(wb_c, wb_raw, 2)
-        y_full(0)
-        round_x(1,0,384)
-        quant_h(0)
-        quant_x(1,0)
-        h_pass(1,0)
-        deal_fp4_words(up_c, up_raw, 0)
-        round_x(1,1,0)
-        deal_scales(up_s, ups_raw)
-        y_low(0)
-        quant_x(1,1)
-        h_pass(1,1)
-        round_x(1,2,256)
-        quant_x(1,2)
-        h_pass(1,2)
-        round_h(1)
-        scale_y(0)
-        y_full(1)
-        add_pair(0,0)
-        quant_h(1)
-        y_low(1)
-        add_pair(0,1)
-        round_x(2,0,256)
-        quant_x(2,0)
-        h_pass(2,0)
-        round_out(0,0,nc.scalar.copy)
-        round_x(2,1,256)
-        quant_x(2,1)
-        h_pass(2,1)
-        round_out(0,1,nc.scalar.copy)
-        round_x(2,2,384)
-        quant_x(2,2)
-        quant_out(0)
-        h_pass(2,2)
-        round_h(2)
-        scale_y(1)
-        y_full(2)
-        add_pair(1,0)
-        quant_h(2)
-        y_low(2)
-        add_pair(1,1)
-        round_out_split(1,0)
-        scale_pair(2,0)
-        add_pair(2,0)
-        scale_pair(2,1)
-        quant_out(1)
-        add_pair(2,1)
-        round_out_split(2,320)
-        quant_out(2)
+            quantize(o_c[:, cols(c)], o_s[:, cols(c)], ob[c])
 
         words_out = out_1[0].rearrange("p t j -> p (t j)").bitcast(I32)
 
-        def store_out(c):
-            nc.sync.dma_start(out=rows4(out_0, 0, c), in_=xr_t[c][:])
+        def store_slots(j0, j1):
+            nc.sync.dma_start(out=rows4(out_0)[:, j0:j1, :], in_=xr_t[:, j0:j1, :])
 
-        def store_pair(c, u):
-            nc.sync.dma_start(out=rows4(out_0, 0, c)[:, 2 * u : 2 * u + 2, :], in_=xr_t[c][:, 2 * u : 2 * u + 2, :])
+        def store_words(c0, c1):
+            t = slice(c0 * TC, c1 * TC)
+            nc.sync.dma_start(out=words_out[:, t], in_=o_c[:, t])
 
-        def store_words(c):
-            nc.sync.dma_start(out=words_out[:, cols(c)], in_=o_c[c][:])
+        def store_scales(queue):
+            for q in (0, 2, 1, 3):
+                queue.dma_start(
+                    out=out_2[0, 4 * q : 4 * q + 4, :].bitcast(I32), in_=o_s[32 * q : 32 * q + 4, :].bitcast(I32)
+                )
 
-        store_out(0)
-        store_words(0)
-        store_out(1)
-        store_pair(2,0)
-        store_words(1)
-        store_pair(2,1)
-        store_words(2)
+        for raw in (dns_raw, wbs_raw, ups_raw):
+            nc.vector.memset(raw[:].bitcast(I32), 0)
         for q in range(4):
-            nc.scalar.dma_start(
-                out=out_2[0, 4 * q : 4 * q + 4, :].bitcast(I32), in_=o_s[32 * q : 32 * q + 4, :].bitcast(I32)
-            )
+            load_packed_scales(nc.gpsimd, wbs_raw, wb_scales, q)
+        for q in range(4):
+            load_scales(nc.gpsimd, ups_raw, upw_scales, q)
+        nc.gpsimd.dma_start(out=b_t[:], in_=b.rearrange("(p j) -> p j", j=PACK))
+        load_dn()
+        for q in (0, 2, 1, 3):
+            load_scales(nc.sync, dns_raw, dn_scales, q)
+        load_x(0, 0)
+        load_x(0, 1)
+        load_wb()
+        load_x(0, 2)
+        load_up()
+        for c in (1, 2):
+            for a in range(PASSES):
+                load_x(c, a)
+        for j in range(PACK):
+            load_slots(x0_t, x0, j, j + 1)
+            load_slots(xr_t, xr, j, j + 1)
+
+        for a in range(PASSES):
+            deal_fp4_words(dn_c, dn_raw, a)
+        for a in range(PASSES):
+            deal_scales(dn_s, dns_raw, a)
+        round_x(0, 0, 320)
+        quant_x(0, 0)
+        h_pass(0, 0)
+        round_x(0, 1, 320)
+        quant_x(0, 1)
+        h_pass(0, 1)
+        for a in range(PASSES):
+            deal_fp8_words(wb_c, wb_raw, a)
+        deal_scales(wb_s, wbs_raw, 0)
+        round_x(0, 2, 320)
+        quant_x(0, 2)
+        h_pass(0, 2)
+        round_h(0)
+        deal_fp4_words(up_c, up_raw, 0)
+        deal_scales(up_s, ups_raw, 0)
+        y_base(0, 0, 4)
+        y_base(0, 1, 5)
+        round_x(1, 0, 512)
+        quant_x(1, 0)
+        quant_h(0)
+        h_pass(1, 0)
+        y_low(0, 0)
+        y_low(0, 1)
+        round_x(1, 1, 320)
+        quant_x(1, 1)
+        h_pass(1, 1)
+        round_x(1, 2, 320)
+        quant_x(1, 2)
+        h_pass(1, 2)
+        round_h(1)
+        y_base(1, 0, 6)
+        y_base(1, 1, 7)
+        round_x(2, 0, 512)
+        quant_x(2, 0)
+        quant_h(1)
+        h_pass(2, 0)
+        y_low(1, 0)
+        y_low(1, 1)
+        round_x(2, 1, 320)
+        quant_x(2, 1)
+        h_pass(2, 1)
+        round_x(2, 2, 320)
+        quant_x(2, 2)
+        h_pass(2, 2)
+        scale_y(0, 0)
+        scale_y(1, 0)
+        round_h(2)
+        y_base(2, 0, 4)
+        y_base(2, 1, 6)
+        add_xr(0, 0, 2)
+        scale_y(0, 1)
+        quant_h(2)
+        scale_y(1, 1)
+        y_base(0, 2, 0)
+        y_low(2, 0)
+        y_low(2, 1)
+        y_low(0, 2)
+        y_all(1, 2, 1)
+        y_all(2, 2, 2)
+        y_all(0, 3, 3)
+        y_all(1, 3, 5)
+        y_all(2, 3, 7)
+        add_xr(1, 0, 2)
+        scale_y(2, 0)
+        scale_y(2, 1)
+        add_xr(0, 2, 3)
+        add_xr(1, 2, 3)
+        for c in range(CHUNKS):
+            round_pair(nc.scalar.copy, c, 0, 0, TC)
+        scale_y(0, 2)
+        scale_y(1, 2)
+        scale_y(2, 2)
+        scale_y(0, 3)
+        add_xr(2, 0, 3)
+        scale_y(1, 3)
+        scale_y(2, 3)
+        add_xr(3, 0, 1)
+        add_xr(3, 1, 3)
+        round_pair(nc.scalar.copy, 0, 1, 0, TC)
+        round_pair(nc.vector.tensor_copy, 2, 1, 0, TC)
+        round_pair(nc.scalar.copy, 1, 1, 0, TC)
+        quant_out(0)
+        quant_out(2)
+        quant_out(1)
+        for j in range(PACK):
+            store_slots(j, j + 1)
+        store_words(0, 1)
+        store_words(2, 3)
+        store_words(1, 2)
+        store_scales(nc.scalar)

@@ -22,6 +22,8 @@ PASSES = K // KP
 TC = 512
 CHUNKS = T // TC
 HN = 128
+X_GROUPS = ((0,), (1,), (2,))
+OUT_GROUPS = ((0, 1), (2,))
 
 
 def tile_mix_cross_pl_kernel(
@@ -37,9 +39,11 @@ def tile_mix_cross_pl_kernel(
         def kept(shape, dtype, name):
             return keep.tile(shape, dtype, name=name, align_bytes=64)
 
-        x_raw = {(c, a): kept([P, PACK, TC], F32, f"x_raw{c}{a}") for c in range(CHUNKS) for a in range(PASSES)}
-        x0_t = kept([P, PACK, T], F32, "x0_t")
-        xr_t = kept([P, PACK, T], F32, "xr_t")
+        x_raw = {
+            (g, a): kept([P, PACK, len(g) * TC], F32, f"x_raw{g[0]}{a}") for g in X_GROUPS for a in range(PASSES)
+        }
+        x0_t = {g: kept([P, PACK, len(g) * TC], F32, f"x0_t{g[0]}") for g in OUT_GROUPS}
+        xr_t = {g: kept([P, PACK, len(g) * TC], F32, f"xr_t{g[0]}") for g in OUT_GROUPS}
         b_t = kept([P, PACK], F32, "b_t")
         wb_raw = kept([P, PASSES, N], I32, "wb_raw")
         dn_raw = kept([P, PASSES, 2 * R], U8, "dn_raw")
@@ -63,16 +67,29 @@ def tile_mix_cross_pl_kernel(
         def cols(c):
             return slice(c * TC, (c + 1) * TC)
 
+        def span(g):
+            return slice(g[0] * TC, (g[-1] + 1) * TC)
+
+        def within(groups, c):
+            g = [g for g in groups if c in g][0]
+            return g, (c - g[0]) * TC
+
         def rows4(dram):
             return dram.rearrange("(p j) t -> p j t", j=PACK)
 
-        def load_x(c, a):
-            nc.sync.dma_start(out=x_raw[c, a][:], in_=rows4(x[a * KP : (a + 1) * KP, cols(c)]))
+        def load_x(g, a):
+            nc.sync.dma_start(out=x_raw[g, a][:], in_=rows4(x[a * KP : (a + 1) * KP, span(g)]))
 
         def load_scales(queue, dst, src, q):
             queue.dma_start(
                 out=dst[32 * q : 32 * q + 4].bitcast(I32),
                 in_=src[:, 4 * q : 4 * q + 4, :].rearrange("a r n -> r a n").bitcast(I32),
+            )
+
+        def load_scale_rows(queue, dst, src, r):
+            queue.dma_start(
+                out=dst[r:P:32].bitcast(I32),
+                in_=src[:, r::4, :].rearrange("a q n -> q a n").bitcast(I32),
             )
 
         def load_packed_scales(queue, dst, src, q):
@@ -81,8 +98,8 @@ def tile_mix_cross_pl_kernel(
                 in_=src[:, 4 * q : 4 * q + 4, :].bitcast(I32),
             )
 
-        def load_slots(dst, src, j0, j1):
-            nc.sync.dma_start(out=dst[:, j0:j1, :], in_=rows4(src)[:, j0:j1, :])
+        def load_slots(dst, src, g, j0, j1):
+            nc.sync.dma_start(out=dst[g][:, j0:j1, :], in_=rows4(src[:, span(g)])[:, j0:j1, :])
 
         def load_dn():
             nc.sync.dma_start(out=dn_raw[:].bitcast(I32), in_=dn_words.rearrange("a p n -> p a n").bitcast(I32))
@@ -126,10 +143,11 @@ def tile_mix_cross_pl_kernel(
 
         def round_x(c, a, split):
             xb[c, a] = stage.tile([P, TC, PACK], BF16, name="xb", align_bytes=64)
+            g, base = within(X_GROUPS, c)
             if split < TC:
-                interleave(nc.scalar.copy, xb[c, a], x_raw[c, a], split, TC, 0)
+                interleave(nc.scalar.copy, xb[c, a], x_raw[g, a], split, TC, base)
             if split:
-                interleave(nc.vector.tensor_copy, xb[c, a], x_raw[c, a], 0, split, 0)
+                interleave(nc.vector.tensor_copy, xb[c, a], x_raw[g, a], 0, split, base)
 
         def quant_x(c, a):
             quantize(x_c[c, a][:], x_s[c, a][:], xb[c, a])
@@ -161,9 +179,10 @@ def tile_mix_cross_pl_kernel(
         def quant_h(c):
             quantize(h_c[c][:], h_s[c][:], hb[c])
 
-        def y_base(c, j, bank):
-            ybank[c, j] = psum.tile([P, TC], F32, name=f"bank{bank}")
-            for a in range(PASSES):
+        def y_base(c, j, bank, passes=range(PASSES)):
+            for a in passes:
+                if a == 0:
+                    ybank[c, j] = psum.tile([P, TC], F32, name=f"bank{bank}")
                 nc.tensor.matmul_mx(
                     out=ybank[c, j][:],
                     lhsT=wb_c[:, a, P * j : P * (j + 1)].bitcast(FP8X4),
@@ -190,52 +209,44 @@ def tile_mix_cross_pl_kernel(
             y_low(c, j)
 
         def scale_y(c, j):
+            g, base = within(OUT_GROUPS, c)
             nc.vector.scalar_tensor_tensor(
-                out=x0_t[:, j, cols(c)],
+                out=x0_t[g][:, j, base : base + TC],
                 in0=ybank[c, j][:],
                 scalar=b_t[:, j : j + 1],
-                in1=x0_t[:, j, cols(c)],
+                in1=x0_t[g][:, j, base : base + TC],
                 op0=ADD,
                 op1=MULT,
             )
 
-        def add_xr(j, c0, c1):
-            t = slice(c0 * TC, c1 * TC)
-            nc.vector.tensor_tensor(out=xr_t[:, j, t], in0=x0_t[:, j, t], in1=xr_t[:, j, t], op=ADD)
+        def add_xr(j0, j1, c0, c1, engine=nc.vector):
+            g, base = within(OUT_GROUPS, c0)
+            t = slice(base, base + (c1 - c0) * TC)
+            engine.tensor_tensor(out=xr_t[g][:, j0:j1, t], in0=x0_t[g][:, j0:j1, t], in1=xr_t[g][:, j0:j1, t], op=ADD)
 
         def round_out(c, split):
             ob[c] = stage.tile([P, TC, PACK], BF16, name="ob", bufs=3, align_bytes=64)
+            g, base = within(OUT_GROUPS, c)
             if split < TC:
-                interleave(nc.scalar.copy, ob[c], xr_t, split, TC, c * TC)
+                interleave(nc.scalar.copy, ob[c], xr_t[g], split, TC, base)
             if split:
-                interleave(nc.vector.tensor_copy, ob[c], xr_t, 0, split, c * TC)
-
-        def round_pair(copy, c, u, t0, t1):
-            if c not in ob:
-                ob[c] = stage.tile([P, TC, PACK], BF16, name="ob", bufs=3, align_bytes=64)
-            js = slice(2 * u, 2 * u + 2)
-            copy(
-                out=ob[c][:, t0:t1, js].rearrange("p (g i) j -> p g j i", i=4),
-                in_=xr_t[:, js, c * TC + t0 : c * TC + t1].rearrange("p j (g i) -> p g j i", i=4),
-            )
+                interleave(nc.vector.tensor_copy, ob[c], xr_t[g], 0, split, base)
 
         def quant_out(c):
             quantize(o_c[:, cols(c)], o_s[:, cols(c)], ob[c])
 
         words_out = out_1[0].rearrange("p t j -> p (t j)").bitcast(I32)
 
-        def store_slots(j0, j1):
-            nc.sync.dma_start(out=rows4(out_0)[:, j0:j1, :], in_=xr_t[:, j0:j1, :])
+        def store_slots(g, j0, j1):
+            nc.sync.dma_start(out=rows4(out_0[:, span(g)])[:, j0:j1, :], in_=xr_t[g][:, j0:j1, :])
 
         def store_words(c0, c1):
             t = slice(c0 * TC, c1 * TC)
             nc.sync.dma_start(out=words_out[:, t], in_=o_c[:, t])
 
         def store_scales(queue):
-            for q in (0, 2, 1, 3):
-                queue.dma_start(
-                    out=out_2[0, 4 * q : 4 * q + 4, :].bitcast(I32), in_=o_s[32 * q : 32 * q + 4, :].bitcast(I32)
-                )
+            for r in range(4):
+                queue.dma_start(out=out_2[0, r::4, :].bitcast(I32), in_=o_s[r:P:32, :].bitcast(I32))
 
         for raw in (dns_raw, wbs_raw, ups_raw):
             nc.vector.memset(raw[:].bitcast(I32), 0)
@@ -244,20 +255,26 @@ def tile_mix_cross_pl_kernel(
         for q in range(4):
             load_scales(nc.gpsimd, ups_raw, upw_scales, q)
         nc.gpsimd.dma_start(out=b_t[:], in_=b.rearrange("(p j) -> p j", j=PACK))
+        wide, last = OUT_GROUPS
         load_dn()
-        for q in (0, 2, 1, 3):
-            load_scales(nc.sync, dns_raw, dn_scales, q)
-        load_x(0, 0)
-        load_x(0, 1)
+        for r in range(4):
+            load_scale_rows(nc.sync, dns_raw, dn_scales, r)
+        load_x((0,), 0)
         load_wb()
-        load_x(0, 2)
+        load_x((0,), 1)
+        load_x((0,), 2)
         load_up()
-        for c in (1, 2):
-            for a in range(PASSES):
-                load_x(c, a)
-        for j in range(PACK):
-            load_slots(x0_t, x0, j, j + 1)
-            load_slots(xr_t, xr, j, j + 1)
+        for a in range(PASSES):
+            load_x((1,), a)
+        load_slots(x0_t, x0, wide, 0, 2)
+        load_slots(x0_t, x0, wide, 2, 4)
+        for a in range(PASSES):
+            load_x((2,), a)
+        load_slots(xr_t, xr, wide, 0, 2)
+        load_slots(xr_t, xr, wide, 2, 4)
+        load_slots(x0_t, x0, last, 0, 4)
+        load_slots(xr_t, xr, last, 0, 2)
+        load_slots(xr_t, xr, last, 2, 4)
 
         for a in range(PASSES):
             deal_fp4_words(dn_c, dn_raw, a)
@@ -266,26 +283,30 @@ def tile_mix_cross_pl_kernel(
         round_x(0, 0, 320)
         quant_x(0, 0)
         h_pass(0, 0)
-        round_x(0, 1, 320)
-        quant_x(0, 1)
-        h_pass(0, 1)
         for a in range(PASSES):
             deal_fp8_words(wb_c, wb_raw, a)
         deal_scales(wb_s, wbs_raw, 0)
+        for j in range(PACK):
+            y_base(0, j, 4 + j, (0,))
+        round_x(0, 1, 320)
+        quant_x(0, 1)
+        h_pass(0, 1)
+        for j in range(PACK):
+            y_base(0, j, 4 + j, (1,))
         round_x(0, 2, 320)
         quant_x(0, 2)
         h_pass(0, 2)
         round_h(0)
         deal_fp4_words(up_c, up_raw, 0)
         deal_scales(up_s, ups_raw, 0)
-        y_base(0, 0, 4)
-        y_base(0, 1, 5)
+        for j in range(PACK):
+            y_base(0, j, 4 + j, (2,))
         round_x(1, 0, 512)
         quant_x(1, 0)
         quant_h(0)
         h_pass(1, 0)
-        y_low(0, 0)
-        y_low(0, 1)
+        for j in range(PACK):
+            y_low(0, j)
         round_x(1, 1, 320)
         quant_x(1, 1)
         h_pass(1, 1)
@@ -293,63 +314,57 @@ def tile_mix_cross_pl_kernel(
         quant_x(1, 2)
         h_pass(1, 2)
         round_h(1)
-        y_base(1, 0, 6)
-        y_base(1, 1, 7)
-        round_x(2, 0, 512)
-        quant_x(2, 0)
+        scale_y(0, 0)
+        scale_y(0, 1)
+        y_base(1, 0, 4)
+        y_base(1, 1, 5)
         quant_h(1)
-        h_pass(2, 0)
         y_low(1, 0)
         y_low(1, 1)
-        round_x(2, 1, 320)
+        scale_y(0, 2)
+        scale_y(0, 3)
+        y_all(1, 2, 6)
+        round_x(2, 0, 256)
+        scale_y(1, 0)
+        quant_x(2, 0)
+        y_all(1, 3, 7)
+        h_pass(2, 0)
+        scale_y(1, 1)
+        scale_y(1, 2)
+        y_base(2, 0, 4, (0,))
+        y_base(2, 1, 5, (0,))
+        round_x(2, 1, 256)
+        scale_y(1, 3)
         quant_x(2, 1)
         h_pass(2, 1)
+        y_base(2, 2, 6, (0,))
         round_x(2, 2, 320)
         quant_x(2, 2)
         h_pass(2, 2)
-        scale_y(0, 0)
-        scale_y(1, 0)
         round_h(2)
-        y_base(2, 0, 4)
-        y_base(2, 1, 6)
-        add_xr(0, 0, 2)
-        scale_y(0, 1)
-        quant_h(2)
-        scale_y(1, 1)
-        y_base(0, 2, 0)
-        y_low(2, 0)
-        y_low(2, 1)
-        y_low(0, 2)
-        y_all(1, 2, 1)
-        y_all(2, 2, 2)
-        y_all(0, 3, 3)
-        y_all(1, 3, 5)
-        y_all(2, 3, 7)
-        add_xr(1, 0, 2)
-        scale_y(2, 0)
-        scale_y(2, 1)
-        add_xr(0, 2, 3)
-        add_xr(1, 2, 3)
-        for c in range(CHUNKS):
-            round_pair(nc.scalar.copy, c, 0, 0, TC)
-        scale_y(0, 2)
-        scale_y(1, 2)
-        scale_y(2, 2)
-        scale_y(0, 3)
-        add_xr(2, 0, 3)
-        scale_y(1, 3)
-        scale_y(2, 3)
-        add_xr(3, 0, 1)
-        add_xr(3, 1, 3)
-        round_pair(nc.scalar.copy, 0, 1, 0, TC)
-        round_pair(nc.vector.tensor_copy, 2, 1, 0, TC)
-        round_pair(nc.scalar.copy, 1, 1, 0, TC)
-        quant_out(0)
-        quant_out(2)
-        quant_out(1)
+        y_base(2, 3, 7, (0,))
         for j in range(PACK):
-            store_slots(j, j + 1)
-        store_words(0, 1)
+            y_base(2, j, 4 + j, (1, 2))
+        add_xr(0, 2, 0, 2)
+        add_xr(2, 4, 0, 1)
+        quant_h(2)
+        for j in range(PACK):
+            y_low(2, j)
+        round_out(0, 0)
+        add_xr(2, 4, 1, 2)
+        round_out(1, 0)
+        for j in range(PACK):
+            scale_y(2, j)
+        add_xr(0, 2, 2, 3)
+        quant_out(0)
+        add_xr(2, 4, 2, 3)
+        quant_out(1)
+        round_out(2, 320)
+        quant_out(2)
+        store_slots(wide, 0, 2)
+        store_slots(wide, 2, 4)
+        store_slots(last, 0, 2)
+        store_words(0, 2)
+        store_slots(last, 2, 4)
         store_words(2, 3)
-        store_words(1, 2)
         store_scales(nc.scalar)

@@ -86,12 +86,6 @@ def tile_mix_cross_pl_kernel(
                 in_=src[:, 4 * q : 4 * q + 4, :].rearrange("a r n -> r a n").bitcast(I32),
             )
 
-        def load_scale_rows(queue, dst, src, r):
-            queue.dma_start(
-                out=dst[r:P:32].bitcast(I32),
-                in_=src[:, r::4, :].rearrange("a q n -> q a n").bitcast(I32),
-            )
-
         def load_packed_scales(queue, dst, src, q):
             queue.dma_start(
                 out=dst[32 * q : 32 * q + 4 * PASSES, 0, :].bitcast(I32),
@@ -245,8 +239,10 @@ def tile_mix_cross_pl_kernel(
             nc.sync.dma_start(out=words_out[:, t], in_=o_c[:, t])
 
         def store_scales(queue):
-            for r in range(4):
-                queue.dma_start(out=out_2[0, r::4, :].bitcast(I32), in_=o_s[r:P:32, :].bitcast(I32))
+            for q in (0, 2, 1, 3):
+                queue.dma_start(
+                    out=out_2[0, 4 * q : 4 * q + 4, :].bitcast(I32), in_=o_s[32 * q : 32 * q + 4, :].bitcast(I32)
+                )
 
         for raw in (dns_raw, wbs_raw, ups_raw):
             nc.vector.memset(raw[:].bitcast(I32), 0)
@@ -257,8 +253,8 @@ def tile_mix_cross_pl_kernel(
         nc.gpsimd.dma_start(out=b_t[:], in_=b.rearrange("(p j) -> p j", j=PACK))
         wide, last = OUT_GROUPS
         load_dn()
-        for r in range(4):
-            load_scale_rows(nc.sync, dns_raw, dn_scales, r)
+        for q in range(4):
+            load_scales(nc.sync, dns_raw, dn_scales, q)
         load_x((0,), 0)
         load_wb()
         load_x((0,), 1)

@@ -22,7 +22,7 @@ PASSES = K // KP
 TC = 512
 CHUNKS = T // TC
 HN = 128
-X_GROUPS = ((0,), (1,), (2,))
+X_GROUPS = (((0,), (1, 2)), ((0,), (1,), (2,)), ((0,), (1,), (2,)))
 OUT_GROUPS = ((0, 1), (2,))
 
 
@@ -40,10 +40,11 @@ def tile_mix_cross_pl_kernel(
             return keep.tile(shape, dtype, name=name, align_bytes=64)
 
         x_raw = {
-            (g, a): kept([P, PACK, len(g) * TC], F32, f"x_raw{g[0]}{a}") for g in X_GROUPS for a in range(PASSES)
+            (g, a): kept([P, PACK, len(g) * TC], F32, f"x_raw{g[0]}{a}") for a in range(PASSES) for g in X_GROUPS[a]
         }
         x0_t = {g: kept([P, PACK, len(g) * TC], F32, f"x0_t{g[0]}") for g in OUT_GROUPS}
         xr_t = {g: kept([P, PACK, len(g) * TC], F32, f"xr_t{g[0]}") for g in OUT_GROUPS}
+        y0_t = kept([P, PACK, TC], F32, "y0_t")
         b_t = kept([P, PACK], F32, "b_t")
         wb_raw = kept([P, PASSES, N], I32, "wb_raw")
         dn_raw = kept([P, PASSES, 2 * R], U8, "dn_raw")
@@ -137,7 +138,7 @@ def tile_mix_cross_pl_kernel(
 
         def round_x(c, a, split):
             xb[c, a] = stage.tile([P, TC, PACK], BF16, name="xb", align_bytes=64)
-            g, base = within(X_GROUPS, c)
+            g, base = within(X_GROUPS[a], c)
             if split < TC:
                 interleave(nc.scalar.copy, xb[c, a], x_raw[g, a], split, TC, base)
             if split:
@@ -202,11 +203,14 @@ def tile_mix_cross_pl_kernel(
             y_base(c, j, bank)
             y_low(c, j)
 
+        def park_y0(j):
+            nc.scalar.copy(out=y0_t[:, j, :], in_=ybank[0, j][:])
+
         def scale_y(c, j):
             g, base = within(OUT_GROUPS, c)
             nc.vector.scalar_tensor_tensor(
                 out=x0_t[g][:, j, base : base + TC],
-                in0=ybank[c, j][:],
+                in0=y0_t[:, j, :] if c == 0 else ybank[c, j][:],
                 scalar=b_t[:, j : j + 1],
                 in1=x0_t[g][:, j, base : base + TC],
                 op0=ADD,
@@ -217,6 +221,17 @@ def tile_mix_cross_pl_kernel(
             g, base = within(OUT_GROUPS, c0)
             t = slice(base, base + (c1 - c0) * TC)
             engine.tensor_tensor(out=xr_t[g][:, j0:j1, t], in0=x0_t[g][:, j0:j1, t], in1=xr_t[g][:, j0:j1, t], op=ADD)
+
+        def add_cols(c, t0, t1):
+            g, base = within(OUT_GROUPS, c)
+            t = slice(base + t0, base + t1)
+            nc.vector.tensor_tensor(out=xr_t[g][:, :, t], in0=x0_t[g][:, :, t], in1=xr_t[g][:, :, t], op=ADD)
+
+        def round_cols(copy, c, t0, t1):
+            if c not in ob:
+                ob[c] = stage.tile([P, TC, PACK], BF16, name="ob", bufs=3, align_bytes=64)
+            g, base = within(OUT_GROUPS, c)
+            interleave(copy, ob[c], xr_t[g], t0, t1, base)
 
         def round_out(c, split):
             ob[c] = stage.tile([P, TC, PACK], BF16, name="ob", bufs=3, align_bytes=64)
@@ -253,32 +268,34 @@ def tile_mix_cross_pl_kernel(
         nc.gpsimd.dma_start(out=b_t[:], in_=b.rearrange("(p j) -> p j", j=PACK))
         wide, last = OUT_GROUPS
         load_dn()
+        load_x((0,), 0)
         for q in range(4):
             load_scales(nc.sync, dns_raw, dn_scales, q)
-        load_x((0,), 0)
         load_wb()
         load_x((0,), 1)
         load_x((0,), 2)
         load_up()
-        for a in range(PASSES):
-            load_x((1,), a)
+        load_x((1, 2), 0)
+        load_x((1,), 1)
+        load_x((1,), 2)
         load_slots(x0_t, x0, wide, 0, 2)
         load_slots(x0_t, x0, wide, 2, 4)
-        for a in range(PASSES):
-            load_x((2,), a)
-        load_slots(xr_t, xr, wide, 0, 2)
-        load_slots(xr_t, xr, wide, 2, 4)
+        load_x((2,), 1)
+        load_x((2,), 2)
+        for j in range(PACK):
+            load_slots(xr_t, xr, wide, j, j + 1)
         load_slots(x0_t, x0, last, 0, 4)
         load_slots(xr_t, xr, last, 0, 2)
         load_slots(xr_t, xr, last, 2, 4)
 
         for a in range(PASSES):
             deal_fp4_words(dn_c, dn_raw, a)
-        for a in range(PASSES):
-            deal_scales(dn_s, dns_raw, a)
         round_x(0, 0, 320)
+        deal_scales(dn_s, dns_raw, 0)
         quant_x(0, 0)
         h_pass(0, 0)
+        deal_scales(dn_s, dns_raw, 1)
+        deal_scales(dn_s, dns_raw, 2)
         for a in range(PASSES):
             deal_fp8_words(wb_c, wb_raw, a)
         deal_scales(wb_s, wbs_raw, 0)
@@ -287,80 +304,83 @@ def tile_mix_cross_pl_kernel(
         round_x(0, 1, 320)
         quant_x(0, 1)
         h_pass(0, 1)
-        for j in range(PACK):
-            y_base(0, j, 4 + j, (1,))
         round_x(0, 2, 320)
         quant_x(0, 2)
         h_pass(0, 2)
-        round_h(0)
         deal_fp4_words(up_c, up_raw, 0)
         deal_scales(up_s, ups_raw, 0)
+        round_h(0, (1, 3))
         for j in range(PACK):
-            y_base(0, j, 4 + j, (2,))
-        round_x(1, 0, 512)
-        quant_x(1, 0)
+            y_base(0, j, 4 + j, (1, 2))
         quant_h(0)
-        h_pass(1, 0)
+        round_x(1, 0, 256)
+        quant_x(1, 0)
         for j in range(PACK):
             y_low(0, j)
-        round_x(1, 1, 320)
+        h_pass(1, 0)
+        for j in range(PACK):
+            park_y0(j)
+        round_x(1, 1, 512)
         quant_x(1, 1)
+        for j in range(PACK):
+            y_base(1, j, 4 + j, (0,))
         h_pass(1, 1)
         round_x(1, 2, 320)
         quant_x(1, 2)
         h_pass(1, 2)
+        round_x(2, 0, 256)
         round_h(1)
+        for j in range(PACK):
+            y_base(1, j, 4 + j, (1, 2))
         scale_y(0, 0)
         scale_y(0, 1)
-        y_base(1, 0, 4)
-        y_base(1, 1, 5)
-        quant_h(1)
-        y_low(1, 0)
-        y_low(1, 1)
+        quant_x(2, 0)
         scale_y(0, 2)
         scale_y(0, 3)
-        y_all(1, 2, 6)
-        round_x(2, 0, 256)
-        scale_y(1, 0)
-        quant_x(2, 0)
-        y_all(1, 3, 7)
+        quant_h(1)
+        for j in range(PACK):
+            y_low(1, j)
         h_pass(2, 0)
+        round_x(2, 1, 192)
+        scale_y(1, 0)
         scale_y(1, 1)
-        scale_y(1, 2)
+        quant_x(2, 1)
         y_base(2, 0, 4, (0,))
         y_base(2, 1, 5, (0,))
-        round_x(2, 1, 256)
-        scale_y(1, 3)
-        quant_x(2, 1)
         h_pass(2, 1)
-        y_base(2, 2, 6, (0,))
-        round_x(2, 2, 320)
+        round_x(2, 2, 256)
+        scale_y(1, 2)
         quant_x(2, 2)
+        y_base(2, 0, 4, (1,))
         h_pass(2, 2)
+        scale_y(1, 3)
         round_h(2)
-        y_base(2, 3, 7, (0,))
-        for j in range(PACK):
-            y_base(2, j, 4 + j, (1, 2))
-        add_xr(0, 2, 0, 2)
-        add_xr(2, 4, 0, 1)
+        y_base(2, 0, 4, (2,))
+        y_base(2, 1, 5, (1, 2))
+        y_base(2, 2, 6)
+        y_base(2, 3, 7)
+        add_xr(0, 1, 0, 2)
+        add_xr(1, 2, 0, 2)
+        add_xr(2, 3, 0, 2)
         quant_h(2)
         for j in range(PACK):
             y_low(2, j)
+        add_xr(3, 4, 0, 1)
         round_out(0, 0)
-        add_xr(2, 4, 1, 2)
+        add_xr(3, 4, 1, 2)
         round_out(1, 0)
         for j in range(PACK):
             scale_y(2, j)
         add_xr(0, 2, 2, 3)
-        quant_out(0)
         add_xr(2, 4, 2, 3)
+        quant_out(0)
         quant_out(1)
-        round_out(2, 320)
+        round_out(2, 192)
         quant_out(2)
         store_slots(wide, 0, 2)
         store_slots(wide, 2, 4)
         store_slots(last, 0, 2)
-        store_words(0, 2)
         store_slots(last, 2, 4)
+        store_words(0, 2)
         store_words(2, 3)
         store_scales(nc.scalar)

@@ -37,7 +37,7 @@ def tile_mix_cross_pl_kernel(
         ctx.enter_context(tc.manual_schedule())
 
         def kept(shape, dtype, name):
-            return keep.tile(shape, dtype, name=name, align_bytes=64)
+            return keep.tile(shape, dtype, name=name, align_bytes=256)
 
         x_raw = {
             (g, a): kept([P, PACK, len(g) * TC], F32, f"x_raw{g[0]}{a}") for a in range(PASSES) for g in X_GROUPS[a]
@@ -137,7 +137,7 @@ def tile_mix_cross_pl_kernel(
         xb, hb, ob, hbank, ybank = {}, {}, {}, {}, {}
 
         def round_x(c, a, split):
-            xb[c, a] = stage.tile([P, TC, PACK], BF16, name="xb", align_bytes=64)
+            xb[c, a] = stage.tile([P, TC, PACK], BF16, name="xb", align_bytes=256)
             g, base = within(X_GROUPS[a], c)
             if split < TC:
                 interleave(nc.scalar.copy, xb[c, a], x_raw[g, a], split, TC, base)
@@ -164,7 +164,7 @@ def tile_mix_cross_pl_kernel(
                     )
 
         def round_h(c, on_vector=()):
-            hb[c] = stage.tile([P, TC, PACK], BF16, name="hb", bufs=2, align_bytes=64)
+            hb[c] = stage.tile([P, TC, PACK], BF16, name="hb", bufs=2, align_bytes=256)
             for s in range(TC // HN):
                 copy = nc.vector.tensor_copy if s in on_vector else nc.scalar.copy
                 copy(
@@ -229,12 +229,12 @@ def tile_mix_cross_pl_kernel(
 
         def round_cols(copy, c, t0, t1):
             if c not in ob:
-                ob[c] = stage.tile([P, TC, PACK], BF16, name="ob", bufs=3, align_bytes=64)
+                ob[c] = stage.tile([P, TC, PACK], BF16, name="ob", bufs=3, align_bytes=256)
             g, base = within(OUT_GROUPS, c)
             interleave(copy, ob[c], xr_t[g], t0, t1, base)
 
         def round_out(c, split):
-            ob[c] = stage.tile([P, TC, PACK], BF16, name="ob", bufs=3, align_bytes=64)
+            ob[c] = stage.tile([P, TC, PACK], BF16, name="ob", bufs=3, align_bytes=256)
             g, base = within(OUT_GROUPS, c)
             if split < TC:
                 interleave(nc.scalar.copy, ob[c], xr_t[g], split, TC, base)

@@ -23,7 +23,10 @@ TC = 512
 CHUNKS = T // TC
 HN = 128
 X_GROUPS = (((0,), (1, 2)), ((0,), (1,), (2,)), ((0,), (1,), (2,)))
-OUT_GROUPS = ((0, 1), (2,))
+X0_GROUPS = ((0, 1), (2,))
+XR_GROUPS = ((0, 1), (2,))
+XB_BUFS = 3
+OB_BUFS = 3
 
 
 def tile_mix_cross_pl_kernel(
@@ -42,9 +45,9 @@ def tile_mix_cross_pl_kernel(
         x_raw = {
             (g, a): kept([P, PACK, len(g) * TC], F32, f"x_raw{g[0]}{a}") for a in range(PASSES) for g in X_GROUPS[a]
         }
-        x0_t = {g: kept([P, PACK, len(g) * TC], F32, f"x0_t{g[0]}") for g in OUT_GROUPS}
-        xr_t = {g: kept([P, PACK, len(g) * TC], F32, f"xr_t{g[0]}") for g in OUT_GROUPS}
-        y0_t = kept([P, PACK, TC], F32, "y0_t")
+        x0_t = {g: kept([P, PACK, len(g) * TC], F32, f"x0_t{g[0]}") for g in X0_GROUPS}
+        xr_t = {g: kept([P, PACK, len(g) * TC], F32, f"xr_t{g[0]}") for g in XR_GROUPS}
+        res = kept([P, PACK, TC], F32, "res")
         b_t = kept([P, PACK], F32, "b_t")
         wb_raw = kept([P, PASSES, N], I32, "wb_raw")
         dn_raw = kept([P, PASSES, 2 * R], U8, "dn_raw")
@@ -65,9 +68,6 @@ def tile_mix_cross_pl_kernel(
         o_c = kept([P, T], I32, "o_c")
         o_s = kept([P, T], U8, "o_s")
 
-        def cols(c):
-            return slice(c * TC, (c + 1) * TC)
-
         def span(g):
             return slice(g[0] * TC, (g[-1] + 1) * TC)
 
@@ -87,6 +87,11 @@ def tile_mix_cross_pl_kernel(
                 in_=src[:, 4 * q : 4 * q + 4, :].rearrange("a r n -> r a n").bitcast(I32),
             )
 
+        def load_scales_across(dst, src, r):
+            nc.sync.dma_start(
+                out=dst[r::32].bitcast(I32), in_=src[:, r::4, :].rearrange("a q n -> q a n").bitcast(I32)
+            )
+
         def load_packed_scales(queue, dst, src, q):
             queue.dma_start(
                 out=dst[32 * q : 32 * q + 4 * PASSES, 0, :].bitcast(I32),
@@ -99,8 +104,10 @@ def tile_mix_cross_pl_kernel(
         def load_dn():
             nc.sync.dma_start(out=dn_raw[:].bitcast(I32), in_=dn_words.rearrange("a p n -> p a n").bitcast(I32))
 
-        def load_wb():
-            nc.sync.dma_start(out=wb_raw[:], in_=wb_words.rearrange("a p n i -> p a (n i)").bitcast(I32))
+        def load_wb(a0, a1):
+            nc.sync.dma_start(
+                out=wb_raw[:, a0:a1, :], in_=wb_words[a0:a1].rearrange("a p n i -> p a (n i)").bitcast(I32)
+            )
 
         def load_up():
             nc.sync.dma_start(out=up_raw[:].bitcast(I32), in_=upw_words.rearrange("a p n -> p a n").bitcast(I32))
@@ -129,28 +136,33 @@ def tile_mix_cross_pl_kernel(
                 in_=src[:, :, base + t0 : base + t1].rearrange("p j (g i) -> p g j i", i=4),
             )
 
-        def quantize(codes, scales, rounded):
+        def quantize(codes, scales, rounded, t0, t1, base=0):
             nc.vector.quantize_mx(
-                out=codes.bitcast(FP8X4), scales=scales, in_=rounded[:].rearrange("p t j -> p (t j)")
+                out=codes[:, base + t0 : base + t1].bitcast(FP8X4),
+                scales=scales[:, base + t0 : base + t1],
+                in_=rounded[:, t0:t1, :].rearrange("p t j -> p (t j)"),
             )
 
         xb, hb, ob, hbank, ybank = {}, {}, {}, {}, {}
+        on_vector, on_scalar = nc.vector.tensor_copy, nc.scalar.copy
 
-        def round_x(c, a, split):
-            xb[c, a] = stage.tile([P, TC, PACK], BF16, name="xb", align_bytes=256)
+        def round_x(copy, c, a, t0=0, t1=TC):
+            if (c, a) not in xb:
+                xb[c, a] = stage.tile([P, TC, PACK], BF16, name="xb", bufs=XB_BUFS, align_bytes=256)
             g, base = within(X_GROUPS[a], c)
-            if split < TC:
-                interleave(nc.scalar.copy, xb[c, a], x_raw[g, a], split, TC, base)
-            if split:
-                interleave(nc.vector.tensor_copy, xb[c, a], x_raw[g, a], 0, split, base)
+            interleave(copy, xb[c, a], x_raw[g, a], t0, t1, base)
 
-        def quant_x(c, a):
-            quantize(x_c[c, a][:], x_s[c, a][:], xb[c, a])
+        def share_x(c, a, split):
+            round_x(on_scalar, c, a, split, TC)
+            round_x(on_vector, c, a, 0, split)
 
-        def h_pass(c, a, bank0=0):
-            for s in range(TC // HN):
-                if a == 0:
-                    hbank[c, s] = psum.tile([P, PACK, HN], F32, name=f"bank{bank0 + s}")
+        def quant_x(c, a, t0=0, t1=TC):
+            quantize(x_c[c, a], x_s[c, a], xb[c, a], t0, t1)
+
+        def h_pass(c, a, banks=range(TC // HN), first=0, last=PASSES - 1):
+            for s in banks:
+                if a == first:
+                    hbank[c, s] = psum.tile([P, PACK, HN], F32, name=f"bank{s}")
                 t = slice(s * HN, (s + 1) * HN)
                 for j in range(PACK):
                     nc.tensor.matmul_mx(
@@ -159,106 +171,94 @@ def tile_mix_cross_pl_kernel(
                         lhsT_scale=dn_s[:, a, P * j : P * (j + 1)],
                         rhs=x_c[c, a][:, t].bitcast(FP8X4),
                         rhs_scale=x_s[c, a][:, t],
-                        start=(a == 0 and j == 0),
-                        stop=(a == PASSES - 1 and j == PACK - 1),
+                        start=(a == first and j == 0),
+                        stop=(a == last and j == PACK - 1),
                     )
 
-        def round_h(c, on_vector=()):
-            hb[c] = stage.tile([P, TC, PACK], BF16, name="hb", bufs=2, align_bytes=256)
-            for s in range(TC // HN):
-                copy = nc.vector.tensor_copy if s in on_vector else nc.scalar.copy
-                copy(
-                    out=hb[c][:, s * HN : (s + 1) * HN, :], in_=hbank[c, s][:].rearrange("p j t -> p t j")
-                )
+        def round_h(copy, c, banks=range(TC // HN)):
+            if c not in hb:
+                hb[c] = stage.tile([P, TC, PACK], BF16, name="hb", bufs=2, align_bytes=256)
+            for s in banks:
+                copy(out=hb[c][:, s * HN : (s + 1) * HN, :], in_=hbank[c, s][:].rearrange("p j t -> p t j"))
 
-        def quant_h(c):
-            quantize(h_c[c][:], h_s[c][:], hb[c])
+        def quant_h(c, t0=0, t1=TC):
+            quantize(h_c[c], h_s[c], hb[c], t0, t1)
 
-        def y_base(c, j, bank, passes=range(PASSES)):
-            for a in passes:
-                if a == 0:
-                    ybank[c, j] = psum.tile([P, TC], F32, name=f"bank{bank}")
+        def y_base(c, a, slots=range(PACK), first=0):
+            for j in slots:
+                if a == first:
+                    ybank[c, j] = psum.tile([P, TC], F32, name=f"bank{PACK + j}")
                 nc.tensor.matmul_mx(
                     out=ybank[c, j][:],
                     lhsT=wb_c[:, a, P * j : P * (j + 1)].bitcast(FP8X4),
                     lhsT_scale=wb_s[4 * a :, 0, P * j : P * (j + 1)],
                     rhs=x_c[c, a][:].bitcast(FP8X4),
                     rhs_scale=x_s[c, a][:],
-                    start=(a == 0),
+                    start=(a == first),
                     stop=False,
                 )
 
-        def y_low(c, j):
-            nc.tensor.matmul_mx(
-                out=ybank[c, j][:],
-                lhsT=up_c[:, 0, 2 * P * j : 2 * P * (j + 1)].bitcast(FP4X4),
-                lhsT_scale=up_s[:, 0, P * j : P * (j + 1)],
-                rhs=h_c[c][:].bitcast(FP8X4),
-                rhs_scale=h_s[c][:],
-                start=False,
-                stop=True,
-            )
+        def y_low(c, slots=range(PACK)):
+            for j in slots:
+                nc.tensor.matmul_mx(
+                    out=ybank[c, j][:],
+                    lhsT=up_c[:, 0, 2 * P * j : 2 * P * (j + 1)].bitcast(FP4X4),
+                    lhsT_scale=up_s[:, 0, P * j : P * (j + 1)],
+                    rhs=h_c[c][:].bitcast(FP8X4),
+                    rhs_scale=h_s[c][:],
+                    start=False,
+                    stop=True,
+                )
 
-        def y_all(c, j, bank):
-            y_base(c, j, bank)
-            y_low(c, j)
+        parked = set()
 
-        def park_y0(j):
-            nc.scalar.copy(out=y0_t[:, j, :], in_=ybank[0, j][:])
+        def park(c, slots=range(PACK)):
+            for j in slots:
+                parked.add((c, j))
+                nc.scalar.copy(out=res[:, j, c * TC : (c + 1) * TC], in_=ybank[c, j][:])
 
         def scale_y(c, j):
-            g, base = within(OUT_GROUPS, c)
+            g, base = within(X0_GROUPS, c)
             nc.vector.scalar_tensor_tensor(
                 out=x0_t[g][:, j, base : base + TC],
-                in0=y0_t[:, j, :] if c == 0 else ybank[c, j][:],
+                in0=res[:, j, c * TC : (c + 1) * TC] if (c, j) in parked else ybank[c, j][:],
                 scalar=b_t[:, j : j + 1],
                 in1=x0_t[g][:, j, base : base + TC],
                 op0=ADD,
                 op1=MULT,
             )
 
-        def add_xr(j0, j1, c0, c1, engine=nc.vector):
-            g, base = within(OUT_GROUPS, c0)
-            t = slice(base, base + (c1 - c0) * TC)
-            engine.tensor_tensor(out=xr_t[g][:, j0:j1, t], in0=x0_t[g][:, j0:j1, t], in1=xr_t[g][:, j0:j1, t], op=ADD)
+        def add_xr(j0, j1, t0, t1, engine=nc.vector):
+            g0, g1 = within(X0_GROUPS, t0 // TC)[0], within(XR_GROUPS, t0 // TC)[0]
+            engine.tensor_tensor(
+                out=xr_t[g1][:, j0:j1, t0 - g1[0] * TC : t1 - g1[0] * TC],
+                in0=x0_t[g0][:, j0:j1, t0 - g0[0] * TC : t1 - g0[0] * TC],
+                in1=xr_t[g1][:, j0:j1, t0 - g1[0] * TC : t1 - g1[0] * TC],
+                op=ADD,
+            )
 
-        def add_cols(c, t0, t1):
-            g, base = within(OUT_GROUPS, c)
-            t = slice(base + t0, base + t1)
-            nc.vector.tensor_tensor(out=xr_t[g][:, :, t], in0=x0_t[g][:, :, t], in1=xr_t[g][:, :, t], op=ADD)
-
-        def round_cols(copy, c, t0, t1):
+        def round_out(copy, c, t0=0, t1=TC):
             if c not in ob:
-                ob[c] = stage.tile([P, TC, PACK], BF16, name="ob", bufs=3, align_bytes=256)
-            g, base = within(OUT_GROUPS, c)
+                ob[c] = stage.tile([P, TC, PACK], BF16, name="ob", bufs=OB_BUFS, align_bytes=256)
+            g, base = within(XR_GROUPS, c)
             interleave(copy, ob[c], xr_t[g], t0, t1, base)
 
-        def round_out(c, split):
-            ob[c] = stage.tile([P, TC, PACK], BF16, name="ob", bufs=3, align_bytes=256)
-            g, base = within(OUT_GROUPS, c)
-            if split < TC:
-                interleave(nc.scalar.copy, ob[c], xr_t[g], split, TC, base)
-            if split:
-                interleave(nc.vector.tensor_copy, ob[c], xr_t[g], 0, split, base)
-
-        def quant_out(c):
-            quantize(o_c[:, cols(c)], o_s[:, cols(c)], ob[c])
+        def quant_out(c, t0=0, t1=TC):
+            quantize(o_c, o_s, ob[c], t0, t1, c * TC)
 
         words_out = out_1[0].rearrange("p t j -> p (t j)").bitcast(I32)
 
         def store_slots(g, j0, j1):
             nc.sync.dma_start(out=rows4(out_0[:, span(g)])[:, j0:j1, :], in_=xr_t[g][:, j0:j1, :])
 
-        def store_words(c0, c1):
-            t = slice(c0 * TC, c1 * TC)
-            nc.sync.dma_start(out=words_out[:, t], in_=o_c[:, t])
+        def store_words(t0, t1):
+            nc.sync.dma_start(out=words_out[:, t0:t1], in_=o_c[:, t0:t1])
 
-        def store_scales(queue):
-            for q in (0, 2, 1, 3):
-                queue.dma_start(
-                    out=out_2[0, 4 * q : 4 * q + 4, :].bitcast(I32), in_=o_s[32 * q : 32 * q + 4, :].bitcast(I32)
-                )
+        def store_scales(queue, t0, t1):
+            for r in range(4):
+                queue.dma_start(out=out_2[0, r::4, t0:t1].bitcast(I32), in_=o_s[r::32, t0:t1].bitcast(I32))
 
+        wide, last = XR_GROUPS
         for raw in (dns_raw, wbs_raw, ups_raw):
             nc.vector.memset(raw[:].bitcast(I32), 0)
         for q in range(4):
@@ -266,14 +266,14 @@ def tile_mix_cross_pl_kernel(
         for q in range(4):
             load_scales(nc.gpsimd, ups_raw, upw_scales, q)
         nc.gpsimd.dma_start(out=b_t[:], in_=b.rearrange("(p j) -> p j", j=PACK))
-        wide, last = OUT_GROUPS
         load_dn()
         load_x((0,), 0)
-        for q in range(4):
-            load_scales(nc.sync, dns_raw, dn_scales, q)
-        load_wb()
+        for r in range(4):
+            load_scales_across(dns_raw, dn_scales, r)
+        load_wb(0, 1)
         load_x((0,), 1)
         load_x((0,), 2)
+        load_wb(1, 3)
         load_up()
         load_x((1, 2), 0)
         load_x((1,), 1)
@@ -290,97 +290,104 @@ def tile_mix_cross_pl_kernel(
 
         for a in range(PASSES):
             deal_fp4_words(dn_c, dn_raw, a)
-        round_x(0, 0, 320)
+        round_x(on_scalar, 0, 0, 256, 512)
+        round_x(on_vector, 0, 0, 0, 256)
         deal_scales(dn_s, dns_raw, 0)
-        quant_x(0, 0)
+        quant_x(0, 0, 0, 256)
+        quant_x(0, 0, 256, 512)
         h_pass(0, 0)
-        deal_scales(dn_s, dns_raw, 1)
-        deal_scales(dn_s, dns_raw, 2)
-        for a in range(PASSES):
-            deal_fp8_words(wb_c, wb_raw, a)
+        deal_fp8_words(wb_c, wb_raw, 0)
         deal_scales(wb_s, wbs_raw, 0)
-        for j in range(PACK):
-            y_base(0, j, 4 + j, (0,))
-        round_x(0, 1, 320)
+        deal_scales(dn_s, dns_raw, 1)
+        y_base(0, 0)
+        share_x(0, 1, 256)
+        deal_scales(dn_s, dns_raw, 2)
         quant_x(0, 1)
         h_pass(0, 1)
-        round_x(0, 2, 320)
+        share_x(0, 2, 256)
+        deal_fp8_words(wb_c, wb_raw, 1)
         quant_x(0, 2)
         h_pass(0, 2)
+        deal_fp8_words(wb_c, wb_raw, 2)
         deal_fp4_words(up_c, up_raw, 0)
+        round_h(on_scalar, 0, (0,))
+        round_h(on_vector, 0, (1,))
+        round_h(on_scalar, 0, (2,))
         deal_scales(up_s, ups_raw, 0)
-        round_h(0, (1, 3))
-        for j in range(PACK):
-            y_base(0, j, 4 + j, (1, 2))
+        round_h(on_scalar, 0, (3,))
+        y_base(0, 1)
+        y_base(0, 2)
         quant_h(0)
-        round_x(1, 0, 256)
+        share_x(1, 0, 320)
         quant_x(1, 0)
-        for j in range(PACK):
-            y_low(0, j)
+        y_low(0)
         h_pass(1, 0)
-        for j in range(PACK):
-            park_y0(j)
-        round_x(1, 1, 512)
+        park(0)
+        round_x(on_vector, 1, 1)
         quant_x(1, 1)
-        for j in range(PACK):
-            y_base(1, j, 4 + j, (0,))
+        y_base(1, 0)
         h_pass(1, 1)
-        round_x(1, 2, 320)
+        share_x(1, 2, 320)
         quant_x(1, 2)
         h_pass(1, 2)
-        round_x(2, 0, 256)
-        round_h(1)
-        for j in range(PACK):
-            y_base(1, j, 4 + j, (1, 2))
+        round_x(on_scalar, 2, 0, 128, 512)
+        round_x(on_vector, 2, 0, 0, 128)
+        round_h(on_scalar, 1)
+        y_base(1, 1)
+        y_base(1, 2)
         scale_y(0, 0)
         scale_y(0, 1)
         quant_x(2, 0)
         scale_y(0, 2)
         scale_y(0, 3)
         quant_h(1)
-        for j in range(PACK):
-            y_low(1, j)
+        y_low(1)
         h_pass(2, 0)
-        round_x(2, 1, 192)
+        share_x(2, 1, 128)
         scale_y(1, 0)
         scale_y(1, 1)
-        quant_x(2, 1)
-        y_base(2, 0, 4, (0,))
-        y_base(2, 1, 5, (0,))
-        h_pass(2, 1)
-        round_x(2, 2, 256)
         scale_y(1, 2)
-        quant_x(2, 2)
-        y_base(2, 0, 4, (1,))
-        h_pass(2, 2)
+        quant_x(2, 1)
+        y_base(2, 0, (0, 1))
+        h_pass(2, 1)
+        share_x(2, 2, 192)
         scale_y(1, 3)
-        round_h(2)
-        y_base(2, 0, 4, (2,))
-        y_base(2, 1, 5, (1, 2))
-        y_base(2, 2, 6)
-        y_base(2, 3, 7)
-        add_xr(0, 1, 0, 2)
-        add_xr(1, 2, 0, 2)
-        add_xr(2, 3, 0, 2)
+        quant_x(2, 2)
+        y_base(2, 1, (0,))
+        h_pass(2, 2)
+        round_h(on_scalar, 2)
+        y_base(2, 2, (0,))
+        y_base(2, 1, (1,))
+        y_base(2, 2, (1,))
+        for a in range(PASSES):
+            y_base(2, a, (2,))
+        add_xr(0, 1, 0, 2 * TC)
+        add_xr(1, 2, 0, 2 * TC)
+        add_xr(2, 3, 0, 2 * TC)
+        add_xr(3, 4, 0, TC)
         quant_h(2)
-        for j in range(PACK):
-            y_low(2, j)
-        add_xr(3, 4, 0, 1)
-        round_out(0, 0)
-        add_xr(3, 4, 1, 2)
-        round_out(1, 0)
+        y_base(2, 0, (3,))
+        y_low(2, (0, 1, 2))
+        for a in (1, 2):
+            y_base(2, a, (3,))
+        y_low(2, (3,))
+        round_out(on_scalar, 0)
+        add_xr(3, 4, TC, 2 * TC)
+        round_out(on_scalar, 1)
         for j in range(PACK):
             scale_y(2, j)
-        add_xr(0, 2, 2, 3)
-        add_xr(2, 4, 2, 3)
+        add_xr(0, 1, 2 * TC, T, nc.gpsimd)
+        add_xr(1, 2, 2 * TC, T)
+        add_xr(2, 4, 2 * TC, T)
+        round_out(on_scalar, 2, 192, 512)
         quant_out(0)
         quant_out(1)
-        round_out(2, 192)
+        round_out(on_vector, 2, 0, 192)
         quant_out(2)
         store_slots(wide, 0, 2)
         store_slots(wide, 2, 4)
         store_slots(last, 0, 2)
         store_slots(last, 2, 4)
-        store_words(0, 2)
-        store_words(2, 3)
-        store_scales(nc.scalar)
+        store_words(0, 2 * TC)
+        store_words(2 * TC, T)
+        store_scales(nc.scalar, 0, T)

@@ -248,8 +248,8 @@ def tile_mix_cross_pl_kernel(
 
         words_out = out_1[0].rearrange("p t j -> p (t j)").bitcast(I32)
 
-        def store_slots(g, j0, j1):
-            nc.sync.dma_start(out=rows4(out_0[:, span(g)])[:, j0:j1, :], in_=xr_t[g][:, j0:j1, :])
+        def store_slots(g, j0, j1, queue=nc.sync):
+            queue.dma_start(out=rows4(out_0[:, span(g)])[:, j0:j1, :], in_=xr_t[g][:, j0:j1, :])
 
         def store_words(t0, t1):
             nc.sync.dma_start(out=words_out[:, t0:t1], in_=o_c[:, t0:t1])
@@ -363,6 +363,7 @@ def tile_mix_cross_pl_kernel(
             y_base(2, a, (2,))
         add_xr(0, 1, 0, 2 * TC)
         add_xr(1, 2, 0, 2 * TC)
+        store_slots(wide, 0, 2, nc.scalar)
         add_xr(2, 3, 0, 2 * TC)
         add_xr(3, 4, 0, TC)
         quant_h(2)
@@ -373,21 +374,20 @@ def tile_mix_cross_pl_kernel(
         y_low(2, (3,))
         round_out(on_scalar, 0)
         add_xr(3, 4, TC, 2 * TC)
+        store_slots(wide, 2, 4, nc.scalar)
         round_out(on_scalar, 1)
         for j in range(PACK):
             scale_y(2, j)
         add_xr(0, 1, 2 * TC, T, nc.gpsimd)
         add_xr(1, 2, 2 * TC, T)
         add_xr(2, 4, 2 * TC, T)
+        store_slots(last, 0, 2)
+        store_slots(last, 2, 4, nc.scalar)
         round_out(on_scalar, 2, 192, 512)
         quant_out(0)
         quant_out(1)
         round_out(on_vector, 2, 0, 192)
         quant_out(2)
-        store_slots(wide, 0, 2)
-        store_slots(wide, 2, 4)
-        store_slots(last, 0, 2)
-        store_slots(last, 2, 4)
         store_words(0, 2 * TC)
         store_words(2 * TC, T)
         store_scales(nc.scalar, 0, T)

@@ -374,7 +374,7 @@ def tile_mix_cross_pl_kernel(
         y_low(2, (3,))
         round_out(on_scalar, 0)
         add_xr(3, 4, TC, 2 * TC)
-        store_slots(wide, 2, 4, nc.scalar)
+        store_slots(wide, 2, 4)
         round_out(on_scalar, 1)
         for j in range(PACK):
             scale_y(2, j)
@@ -382,7 +382,7 @@ def tile_mix_cross_pl_kernel(
         add_xr(1, 2, 2 * TC, T)
         add_xr(2, 4, 2 * TC, T)
         store_slots(last, 0, 2)
-        store_slots(last, 2, 4, nc.scalar)
+        store_slots(last, 2, 4)
         round_out(on_scalar, 2, 192, 512)
         quant_out(0)
         quant_out(1)

from contextlib import ExitStack

import concourse.mybir as mybir

K, R, N, T = 1536, 512, 512, 1536
FLOPS = 2 * T * (K * R + K * N + R * N)

F32 = mybir.dt.float32
BF16 = mybir.dt.bfloat16
I32 = mybir.dt.int32
U16 = mybir.dt.uint16
U8 = mybir.dt.uint8
FP8X4 = mybir.dt.float8_e4m3fn_x4
FP4X4 = mybir.dt.float4_e2m1fn_x4
ADD = mybir.AluOpType.add
MULT = mybir.AluOpType.mult

P = 128
PACK = 4
KP = P * PACK
PASSES = K // KP
TC = 512
CHUNKS = T // TC
HN = 128
X_GROUPS = (((0,), (1, 2)), ((0,), (1,), (2,)), ((0,), (1,), (2,)))
X0_GROUPS = ((0, 1), (2,))
XR_GROUPS = ((0, 1), (2,))
XB_BUFS = 3
OB_BUFS = 3


def tile_mix_cross_pl_kernel(
    tc, x, wb_words, wb_scales, dn_words, dn_scales, upw_words, upw_scales, x0, b, xr, out_0, out_1, out_2
):
    nc = tc.nc
    with ExitStack() as ctx:
        keep = ctx.enter_context(tc.tile_pool(name="keep", bufs=1))
        stage = ctx.enter_context(tc.tile_pool(name="stage", bufs=3))
        psum = ctx.enter_context(tc.psum_pool(name="psum", bufs=1))
        ctx.enter_context(tc.manual_schedule())

        def kept(shape, dtype, name):
            return keep.tile(shape, dtype, name=name, align_bytes=256)

        x_raw = {
            (g, a): kept([P, PACK, len(g) * TC], F32, f"x_raw{g[0]}{a}") for a in range(PASSES) for g in X_GROUPS[a]
        }
        x0_t = {g: kept([P, PACK, len(g) * TC], F32, f"x0_t{g[0]}") for g in X0_GROUPS}
        xr_t = {g: kept([P, PACK, len(g) * TC], F32, f"xr_t{g[0]}") for g in XR_GROUPS}
        res = kept([P, PACK, TC], F32, "res")
        b_t = kept([P, PACK], F32, "b_t")
        wb_raw = kept([P, PASSES, N], I32, "wb_raw")
        dn_raw = kept([P, PASSES, 2 * R], U8, "dn_raw")
        up_raw = kept([P, 1, 2 * N], U8, "up_raw")
        wbs_raw = kept([P, 1, N], U8, "wbs_raw")
        dns_raw = kept([P, PASSES, R], U8, "dns_raw")
        ups_raw = kept([P, 1, N], U8, "ups_raw")
        wb_c = kept([P, PASSES, N], I32, "wb_c")
        dn_c = kept([P, PASSES, 2 * R], U8, "dn_c")
        up_c = kept([P, 1, 2 * N], U8, "up_c")
        wb_s = kept([P, 1, N], U8, "wb_s")
        dn_s = kept([P, PASSES, R], U8, "dn_s")
        up_s = kept([P, 1, N], U8, "up_s")
        x_c = {(c, a): kept([P, TC], I32, f"x_c{c}{a}") for c in range(CHUNKS) for a in range(PASSES)}
        x_s = {(c, a): kept([P, TC], U8, f"x_s{c}{a}") for c in range(CHUNKS) for a in range(PASSES)}
        h_c = [kept([P, TC], I32, f"h_c{c}") for c in range(CHUNKS)]
        h_s = [kept([P, TC], U8, f"h_s{c}") for c in range(CHUNKS)]
        o_c = kept([P, T], I32, "o_c")
        o_s = kept([P, T], U8, "o_s")

        def span(g):
            return slice(g[0] * TC, (g[-1] + 1) * TC)

        def within(groups, c):
            g = [g for g in groups if c in g][0]
            return g, (c - g[0]) * TC

        def rows4(dram):
            return dram.rearrange("(p j) t -> p j t", j=PACK)

        def load_x(g, a):
            nc.sync.dma_start(out=x_raw[g, a][:], in_=rows4(x[a * KP : (a + 1) * KP, span(g)]))

        def load_scales(queue, dst, src, q):
            queue.dma_start(
                out=dst[32 * q : 32 * q + 4].bitcast(I32),
                in_=src[:, 4 * q : 4 * q + 4, :].rearrange("a r n -> r a n").bitcast(I32),
            )

        def load_scales_across(dst, src, r):
            nc.sync.dma_start(
                out=dst[r::32].bitcast(I32), in_=src[:, r::4, :].rearrange("a q n -> q a n").bitcast(I32)
            )

        def load_packed_scales(queue, dst, src, q):
            queue.dma_start(
                out=dst[32 * q : 32 * q + 4 * PASSES, 0, :].bitcast(I32),
                in_=src[:, 4 * q : 4 * q + 4, :].bitcast(I32),
            )

        def load_slots(dst, src, g, j0, j1):
            nc.sync.dma_start(out=dst[g][:, j0:j1, :], in_=rows4(src[:, span(g)])[:, j0:j1, :])

        def load_dn():
            nc.sync.dma_start(out=dn_raw[:].bitcast(I32), in_=dn_words.rearrange("a p n -> p a n").bitcast(I32))

        def load_wb(a0, a1):
            nc.sync.dma_start(
                out=wb_raw[:, a0:a1, :], in_=wb_words[a0:a1].rearrange("a p n i -> p a (n i)").bitcast(I32)
            )

        def load_up():
            nc.sync.dma_start(out=up_raw[:].bitcast(I32), in_=upw_words.rearrange("a p n -> p a n").bitcast(I32))

        def deal_fp8_words(dst, src, a):
            nc.vector.tensor_copy(
                out=dst[:, a, :].rearrange("p (j g m) -> p g j m", j=PACK, m=4),
                in_=src[:, a, :].rearrange("p (g m j) -> p g j m", j=PACK, m=4),
            )

        def deal_fp4_words(dst, src, a):
            nc.vector.tensor_copy(
                out=dst[:, a, :].bitcast(U16).rearrange("p (j g m) -> p g j m", j=PACK, m=8),
                in_=src[:, a, :].bitcast(U16).rearrange("p (g m j) -> p g j m", j=PACK, m=8),
            )

        def deal_scales(dst, src, a):
            nc.vector.tensor_copy(
                out=dst[:, a, :].rearrange("p (j g m) -> p g j m", j=PACK, m=16),
                in_=src[:, a, :].rearrange("p (g m j) -> p g j m", j=PACK, m=16),
            )

        def interleave(copy, dst, src, t0, t1, base):
            copy(
                out=dst[:, t0:t1, :].rearrange("p (g i) j -> p g j i", i=4),
                in_=src[:, :, base + t0 : base + t1].rearrange("p j (g i) -> p g j i", i=4),
            )

        def quantize(codes, scales, rounded, t0, t1, base=0):
            nc.vector.quantize_mx(
                out=codes[:, base + t0 : base + t1].bitcast(FP8X4),
                scales=scales[:, base + t0 : base + t1],
                in_=rounded[:, t0:t1, :].rearrange("p t j -> p (t j)"),
            )

        xb, hb, ob, hbank, ybank = {}, {}, {}, {}, {}
        on_vector, on_scalar = nc.vector.tensor_copy, nc.scalar.copy

        def round_x(copy, c, a, t0=0, t1=TC):
            if (c, a) not in xb:
                xb[c, a] = stage.tile([P, TC, PACK], BF16, name="xb", bufs=XB_BUFS, align_bytes=256)
            g, base = within(X_GROUPS[a], c)
            interleave(copy, xb[c, a], x_raw[g, a], t0, t1, base)

        def share_x(c, a, split):
            round_x(on_scalar, c, a, split, TC)
            round_x(on_vector, c, a, 0, split)

        def quant_x(c, a, t0=0, t1=TC):
            quantize(x_c[c, a], x_s[c, a], xb[c, a], t0, t1)

        def h_pass(c, a, banks=range(TC // HN), first=0, last=PASSES - 1):
            for s in banks:
                if a == first:
                    hbank[c, s] = psum.tile([P, PACK, HN], F32, name=f"bank{s}")
                t = slice(s * HN, (s + 1) * HN)
                for j in range(PACK):
                    nc.tensor.matmul_mx(
                        out=hbank[c, s][:, j, :],
                        lhsT=dn_c[:, a, 2 * P * j : 2 * P * (j + 1)].bitcast(FP4X4),
                        lhsT_scale=dn_s[:, a, P * j : P * (j + 1)],
                        rhs=x_c[c, a][:, t].bitcast(FP8X4),
                        rhs_scale=x_s[c, a][:, t],
                        start=(a == first and j == 0),
                        stop=(a == last and j == PACK - 1),
                    )

        def round_h(copy, c, banks=range(TC // HN)):
            if c not in hb:
                hb[c] = stage.tile([P, TC, PACK], BF16, name="hb", bufs=2, align_bytes=256)
            for s in banks:
                copy(out=hb[c][:, s * HN : (s + 1) * HN, :], in_=hbank[c, s][:].rearrange("p j t -> p t j"))

        def quant_h(c, t0=0, t1=TC):
            quantize(h_c[c], h_s[c], hb[c], t0, t1)

        def y_base(c, a, slots=range(PACK), first=0):
            for j in slots:
                if a == first:
                    ybank[c, j] = psum.tile([P, TC], F32, name=f"bank{PACK + j}")
                nc.tensor.matmul_mx(
                    out=ybank[c, j][:],
                    lhsT=wb_c[:, a, P * j : P * (j + 1)].bitcast(FP8X4),
                    lhsT_scale=wb_s[4 * a :, 0, P * j : P * (j + 1)],
                    rhs=x_c[c, a][:].bitcast(FP8X4),
                    rhs_scale=x_s[c, a][:],
                    start=(a == first),
                    stop=False,
                )

        def y_low(c, slots=range(PACK)):
            for j in slots:
                nc.tensor.matmul_mx(
                    out=ybank[c, j][:],
                    lhsT=up_c[:, 0, 2 * P * j : 2 * P * (j + 1)].bitcast(FP4X4),
                    lhsT_scale=up_s[:, 0, P * j : P * (j + 1)],
                    rhs=h_c[c][:].bitcast(FP8X4),
                    rhs_scale=h_s[c][:],
                    start=False,
                    stop=True,
                )

        parked = set()

        def park(c, slots=range(PACK)):
            for j in slots:
                parked.add((c, j))
                nc.scalar.copy(out=res[:, j, c * TC : (c + 1) * TC], in_=ybank[c, j][:])

        def scale_y(c, j):
            g, base = within(X0_GROUPS, c)
            nc.vector.scalar_tensor_tensor(
                out=x0_t[g][:, j, base : base + TC],
                in0=res[:, j, c * TC : (c + 1) * TC] if (c, j) in parked else ybank[c, j][:],
                scalar=b_t[:, j : j + 1],
                in1=x0_t[g][:, j, base : base + TC],
                op0=ADD,
                op1=MULT,
            )

        def add_xr(j0, j1, t0, t1, engine=nc.vector):
            g0, g1 = within(X0_GROUPS, t0 // TC)[0], within(XR_GROUPS, t0 // TC)[0]
            engine.tensor_tensor(
                out=xr_t[g1][:, j0:j1, t0 - g1[0] * TC : t1 - g1[0] * TC],
                in0=x0_t[g0][:, j0:j1, t0 - g0[0] * TC : t1 - g0[0] * TC],
                in1=xr_t[g1][:, j0:j1, t0 - g1[0] * TC : t1 - g1[0] * TC],
                op=ADD,
            )

        def round_out(copy, c, t0=0, t1=TC):
            if c not in ob:
                ob[c] = stage.tile([P, TC, PACK], BF16, name="ob", bufs=OB_BUFS, align_bytes=256)
            g, base = within(XR_GROUPS, c)
            interleave(copy, ob[c], xr_t[g], t0, t1, base)

        def quant_out(c, t0=0, t1=TC):
            quantize(o_c, o_s, ob[c], t0, t1, c * TC)

        words_out = out_1[0].rearrange("p t j -> p (t j)").bitcast(I32)

        def store_slots(g, j0, j1, queue=nc.sync):
            queue.dma_start(out=rows4(out_0[:, span(g)])[:, j0:j1, :], in_=xr_t[g][:, j0:j1, :])

        def store_words(t0, t1):
            nc.sync.dma_start(out=words_out[:, t0:t1], in_=o_c[:, t0:t1])

        def store_scales(queue, t0, t1):
            for r in range(4):
                queue.dma_start(out=out_2[0, r::4, t0:t1].bitcast(I32), in_=o_s[r::32, t0:t1].bitcast(I32))

        wide, last = XR_GROUPS
        for raw in (dns_raw, wbs_raw, ups_raw):
            nc.vector.memset(raw[:].bitcast(I32), 0)
        for q in range(4):
            load_packed_scales(nc.gpsimd, wbs_raw, wb_scales, q)
        for q in range(4):
            load_scales(nc.gpsimd, ups_raw, upw_scales, q)
        nc.gpsimd.dma_start(out=b_t[:], in_=b.rearrange("(p j) -> p j", j=PACK))
        load_dn()
        load_x((0,), 0)
        for r in range(4):
            load_scales_across(dns_raw, dn_scales, r)
        load_wb(0, 1)
        load_x((0,), 1)
        load_x((0,), 2)
        load_wb(1, 3)
        load_up()
        load_x((1, 2), 0)
        load_x((1,), 1)
        load_x((1,), 2)
        load_slots(x0_t, x0, wide, 0, 2)
        load_slots(x0_t, x0, wide, 2, 4)
        load_x((2,), 1)
        load_x((2,), 2)
        for j in range(PACK):
            load_slots(xr_t, xr, wide, j, j + 1)
        load_slots(x0_t, x0, last, 0, 4)
        load_slots(xr_t, xr, last, 0, 2)
        load_slots(xr_t, xr, last, 2, 4)

        for a in range(PASSES):
            deal_fp4_words(dn_c, dn_raw, a)
        round_x(on_scalar, 0, 0, 256, 512)
        round_x(on_vector, 0, 0, 0, 256)
        deal_scales(dn_s, dns_raw, 0)
        quant_x(0, 0, 0, 256)
        quant_x(0, 0, 256, 512)
        h_pass(0, 0)
        deal_fp8_words(wb_c, wb_raw, 0)
        deal_scales(wb_s, wbs_raw, 0)
        deal_scales(dn_s, dns_raw, 1)
        y_base(0, 0)
        share_x(0, 1, 256)
        deal_scales(dn_s, dns_raw, 2)
        quant_x(0, 1)
        h_pass(0, 1)
        share_x(0, 2, 256)
        deal_fp8_words(wb_c, wb_raw, 1)
        quant_x(0, 2)
        h_pass(0, 2)
        deal_fp8_words(wb_c, wb_raw, 2)
        deal_fp4_words(up_c, up_raw, 0)
        round_h(on_scalar, 0, (0,))
        round_h(on_vector, 0, (1,))
        round_h(on_scalar, 0, (2,))
        deal_scales(up_s, ups_raw, 0)
        round_h(on_scalar, 0, (3,))
        y_base(0, 1)
        y_base(0, 2)
        quant_h(0)
        share_x(1, 0, 320)
        quant_x(1, 0)
        y_low(0)
        h_pass(1, 0)
        park(0)
        round_x(on_vector, 1, 1)
        quant_x(1, 1)
        y_base(1, 0)
        h_pass(1, 1)
        share_x(1, 2, 320)
        quant_x(1, 2)
        h_pass(1, 2)
        round_x(on_scalar, 2, 0, 128, 512)
        round_x(on_vector, 2, 0, 0, 128)
        round_h(on_scalar, 1)
        y_base(1, 1)
        y_base(1, 2)
        scale_y(0, 0)
        scale_y(0, 1)
        quant_x(2, 0)
        scale_y(0, 2)
        scale_y(0, 3)
        quant_h(1)
        y_low(1)
        h_pass(2, 0)
        share_x(2, 1, 128)
        scale_y(1, 0)
        scale_y(1, 1)
        scale_y(1, 2)
        quant_x(2, 1)
        y_base(2, 0, (0, 1))
        h_pass(2, 1)
        share_x(2, 2, 192)
        scale_y(1, 3)
        quant_x(2, 2)
        y_base(2, 1, (0,))
        h_pass(2, 2)
        round_h(on_scalar, 2)
        y_base(2, 2, (0,))
        y_base(2, 1, (1,))
        y_base(2, 2, (1,))
        for a in range(PASSES):
            y_base(2, a, (2,))
        add_xr(0, 1, 0, 2 * TC)
        add_xr(1, 2, 0, 2 * TC)
        store_slots(wide, 0, 2, nc.scalar)
        add_xr(2, 3, 0, 2 * TC)
        add_xr(3, 4, 0, TC)
        quant_h(2)
        y_base(2, 0, (3,))
        y_low(2, (0, 1, 2))
        for a in (1, 2):
            y_base(2, a, (3,))
        y_low(2, (3,))
        round_out(on_scalar, 0)
        add_xr(3, 4, TC, 2 * TC)
        store_slots(wide, 2, 4)
        round_out(on_scalar, 1)
        for j in range(PACK):
            scale_y(2, j)
        add_xr(0, 1, 2 * TC, T, nc.gpsimd)
        add_xr(1, 2, 2 * TC, T)
        add_xr(2, 4, 2 * TC, T)
        store_slots(last, 0, 2)
        store_slots(last, 2, 4)
        round_out(on_scalar, 2, 192, 512)
        quant_out(0)
        quant_out(1)
        round_out(on_vector, 2, 0, 192)
        quant_out(2)
        store_words(0, 2 * TC)
        store_words(2 * TC, T)
        store_scales(nc.scalar, 0, T)
